import numpy as np
import ml_dtypes


def mxq(x, axis, fmt="e4m3"):
    dtype, down = {"e4m3": (ml_dtypes.float8_e4m3fn, 7), "e5m2": (ml_dtypes.float8_e5m2, 14)}[fmt]
    v = np.moveaxis(np.asarray(x, np.float32).astype(ml_dtypes.bfloat16).astype(np.float64), axis, -1)
    blocks = v.reshape(v.shape[:-1] + (-1, 32))
    amax = np.abs(blocks).max(-1, keepdims=True)
    byte = np.maximum(np.where(amax > 0, np.frexp(amax)[1] - 1 + 127, 0) - down, 1)
    scale = np.exp2(byte - 127.0)
    codes = (blocks / scale).astype(np.float32).astype(dtype).astype(np.float64)
    return np.moveaxis((codes * scale).reshape(v.shape), -1, axis)


WIDE = False


def mx_kscale(k):
    if not WIDE:
        return np.ones(k)
    levels = np.array([10, -10, 5, -5, 0])
    if k % 512:
        return np.exp2(np.random.permutation(np.resize(levels, k // 32))).repeat(32)
    a = np.empty((k // 512, 16))
    for p in range(k // 512):
        a[p, :8] = np.random.permutation(np.resize(levels, 8))
        for g in range(8):
            far = levels[np.abs(levels - a[p, g]) >= 10]
            a[p, g + 8] = far[np.random.randint(len(far))]
    return np.exp2(a.ravel()).repeat(32)


def f64(x):
    return np.asarray(x).astype(np.float64)


def striped(idx):
    return np.tile(idx.reshape(-1, 16).T, (8, 1)).astype(np.uint16)


def unstriped(offs):
    return offs[:16].T.reshape(-1).astype(np.int64)


E2M1 = np.array([0.0, 0.5, 1.0, 1.5, 2.0, 3.0, 4.0, 6.0, -0.0, -0.5, -1.0, -1.5, -2.0, -3.0, -4.0, -6.0])


def pack_weight(w, fmt):
    k, n = w.shape
    w = f64(np.asarray(w, np.float32).astype(ml_dtypes.bfloat16)).reshape(k // 32, 32, n)
    amax = np.abs(w).max(1)
    if fmt == "e4m3":
        byte = np.frexp(amax)[1] - 1 + 127 - 7
    else:
        mant, ex = np.frexp(amax / 6.0)
        byte = np.where(mant > 0.5, ex, ex - 1) + 127
    byte = np.clip(np.where(amax > 0, byte, 1), 1, 254)
    scaled = (w * np.exp2(127.0 - byte)[:, None, :]).reshape(k, n).astype(np.float32)
    by_word = np.ascontiguousarray(scaled.reshape(k // 512, 128, 4, n).transpose(0, 1, 3, 2))
    if fmt == "e4m3":
        words = by_word.astype(ml_dtypes.float8_e4m3fn).view(np.uint8)
    else:
        c = by_word.astype(ml_dtypes.float4_e2m1fn).view(np.uint8) & 0xF
        words = (c[..., 0::2] | (c[..., 1::2] << 4)).reshape(k // 512, 128, 2 * n)
    return np.ascontiguousarray(words), np.ascontiguousarray(byte.astype(np.uint8).reshape(k // 512, 16, n))


def unpack_weight(words, scales, fmt):
    g, _, n = scales.shape
    words = np.ascontiguousarray(words).reshape(g, 128, n, -1)
    if fmt == "e4m3":
        vals = words.view(ml_dtypes.float8_e4m3fn).astype(np.float64)
    else:
        nib = np.empty((g, 128, n, 4), np.uint8)
        nib[..., 0::2] = words & 0xF
        nib[..., 1::2] = words >> 4
        vals = E2M1[nib]
    vals = vals * np.repeat(np.exp2(scales.astype(np.float64) - 127.0), 8, axis=1)[..., None]
    return vals.transpose(0, 1, 3, 2).reshape(g * 512, n)


def relu(v):
    return np.maximum(v, 0.0)


K, T, E, C, H, N = 512, 1536, 6, 256, 512, 128


def by_expert(wq, xq):
    return np.concatenate([wq[e].T @ xq[:, e * C:(e + 1) * C] for e in range(E)], axis=1)


def setup_inputs():
    n = np.random.standard_normal
    s = mx_kscale(K)
    u = mx_kscale(H)
    slot_token = np.random.permutation(T)[:E * C]
    x = pack_weight(n((K, T)) * s[:, None], "e4m3")
    w1 = pack_weight(n((K, H)) / np.sqrt(K) / s[:, None], "e4m3")
    w3 = pack_weight(n((K, H)) / np.sqrt(K) / s[:, None] * u, "e4m3")
    w2 = [pack_weight(m, "e2m1") for m in n((E, H, N)) / np.sqrt(H) / u[None, :, None]]
    return {
        "x_words": x[0],
        "x_scales": x[1],
        "w1_words": w1[0],
        "w1_scales": w1[1],
        "w3_words": w3[0],
        "w3_scales": w3[1],
        "w2_words": np.stack([m[0] for m in w2]),
        "w2_scales": np.stack([m[1] for m in w2]),
        "gate": np.tile(np.random.uniform(0.2, 1.0, E * C), (128, 1)).astype(np.float32),
        "offs": striped(slot_token),
    }


def reference(x_words, x_scales, w1_words, w1_scales, w3_words, w3_scales, w2_words, w2_scales, gate, offs):
    w1 = unpack_weight(w1_words, w1_scales, "e4m3")
    w3 = unpack_weight(w3_words, w3_scales, "e4m3")
    w2 = np.stack([unpack_weight(w2_words[e], w2_scales[e], "e2m1") for e in range(E)])
    idx = unstriped(offs)
    x = unpack_weight(x_words, x_scales, "e4m3")
    h = relu(w1.T @ x) * (w3.T @ x)
    y = by_expert(w2, mxq(h[:, idx], 0, "e4m3"))
    out = np.zeros((N, T))
    out[:, idx] = f64(gate[:1]) * y
    return out

@@ -1,0 +1,201 @@
+from contextlib import ExitStack
+
+import concourse.mybir as mybir
+
+K, T, E, C, H, N = 512, 1536, 6, 256, 512, 128
+FLOPS = 2 * K * H * T * 2 + 2 * H * N * T
+
+F32 = mybir.dt.float32
+BF16 = mybir.dt.bfloat16
+I32 = mybir.dt.int32
+U32 = mybir.dt.uint32
+U16 = mybir.dt.uint16
+U8 = mybir.dt.uint8
+FP8X4 = mybir.dt.float8_e4m3fn_x4
+FP4X4 = mybir.dt.float4_e2m1fn_x4
+ALU = mybir.AluOpType
+COPY = mybir.ActivationFunctionType.Copy
+
+P = 128
+CHUNK = 512
+HALF = 256
+X_ROW = 0
+W1_ROW = 0
+W3_ROW = H
+
+
+def tile_moe_sup_glu_relu_kernel(
+    tc, x_words, x_scales, w1_words, w1_scales, w3_words, w3_scales, w2_words, w2_scales, gate, offs, out
+):
+    nc = tc.nc
+    with ExitStack() as ctx:
+        keep = ctx.enter_context(tc.tile_pool(name="keep", bufs=1))
+        ring = ctx.enter_context(tc.tile_pool(name="ring", bufs=3))
+        psum_a = ctx.enter_context(tc.psum_pool(name="psum_a", bufs=3))
+        psum_b = ctx.enter_context(tc.psum_pool(name="psum_b", bufs=3))
+        psum_y = ctx.enter_context(tc.psum_pool(name="psum_y", bufs=2))
+
+        offsets = keep.tile([P, T // 16], U16, name="offsets")
+        w1_scale_raw = keep.tile([P, H], U8, name="w1_scale_raw", align_bytes=64)
+        w3_scale_raw = keep.tile([P, H], U8, name="w3_scale_raw", align_bytes=64)
+        w_scale = keep.tile([P, 2 * H], U8, name="w_scale", align_bytes=64)
+        x_scale = keep.tile([P, T], U8, name="x_scale", align_bytes=64)
+        w2_scale = keep.tile([P, E * N], U8, name="w2_scale", align_bytes=64)
+        w1_raw = keep.tile([P, H], I32, name="w1_raw", align_bytes=64)
+        w3_raw = keep.tile([P, H], I32, name="w3_raw", align_bytes=64)
+        w1_code = keep.tile([P, H], I32, name="w1_code", align_bytes=64)
+        w3_code = keep.tile([P, H], I32, name="w3_code", align_bytes=64)
+        x_code = [keep.tile([P, CHUNK], I32, name="x_code%d" % j, align_bytes=64) for j in range(T // CHUNK)]
+        w2_code = keep.tile([P, E * 2 * N], U8, name="w2_code", align_bytes=64)
+        gate_sb = keep.tile([P, T], F32, name="gate_sb", align_bytes=64)
+        h_pair = keep.tile([P, 2 * T], BF16, name="h_pair", align_bytes=64)
+        h_single = [keep.tile([P, T], BF16, name="h_single%d" % t, align_bytes=64) for t in range(2)]
+        result = keep.tile([P, T], F32, name="result", align_bytes=64)
+
+        nc.gpsimd.memset(w2_scale[:].bitcast(I32), 0)
+
+        def load_scale_rows(engine, plane, scales, q):
+            rows = scales[4 * q : 4 * q + 4, :].bitcast(I32)
+            engine.dma_start(
+                out=plane[32 * q : 32 * q + 32, :].bitcast(I32),
+                in_=rows.unsqueeze(0).to_broadcast([8, 4, rows.shape[1]]),
+            )
+
+        def words(ap):
+            return ap.rearrange("p n t -> p (n t)").bitcast(I32)
+
+        xw = words(x_words[0])
+        for q in range(4):
+            load_scale_rows(nc.scalar, w3_scale_raw, w3_scales[0], q)
+        for q in range(2):
+            load_scale_rows(nc.sync, x_scale, x_scales[0], q)
+        nc.sync.dma_start(out=w3_raw[:], in_=words(w3_words[0]))
+        nc.sync.dma_start(out=x_code[0][:], in_=xw[:, 0:CHUNK])
+        for q in range(2, 4):
+            load_scale_rows(nc.sync, x_scale, x_scales[0], q)
+        for q in range(4):
+            load_scale_rows(nc.sync, w1_scale_raw, w1_scales[0], q)
+        nc.sync.dma_start(out=w1_raw[:], in_=words(w1_words[0]))
+        for j in range(1, T // CHUNK):
+            nc.sync.dma_start(out=x_code[j][:], in_=xw[:, j * CHUNK : (j + 1) * CHUNK])
+        nc.sync.dma_start(offsets[:], offs)
+        nc.sync.dma_start(
+            out=w2_code[:].bitcast(I32).rearrange("p (e w) -> p e w", e=E),
+            in_=w2_words.bitcast(I32).rearrange("e s p w -> p (e s) w"),
+        )
+        for q in range(4):
+            nc.sync.dma_start(
+                out=w2_scale[32 * q : 32 * q + 4, :].bitcast(I32).rearrange("r (e w) -> r e w", e=E),
+                in_=w2_scales.bitcast(I32)[:, 0, 4 * q : 4 * q + 4, :].rearrange("e r w -> r e w"),
+            )
+        nc.sync.dma_start(out=gate_sb[:], in_=gate)
+
+        def permute_columns(dst, src):
+            nc.vector.tensor_copy(
+                out=dst.rearrange("p (t m) -> p m t", t=4), in_=src.rearrange("p (m t) -> p m t", t=4)
+            )
+
+        permute_columns(w_scale[:, H : 2 * H], w3_scale_raw[:])
+        permute_columns(w3_code[:], w3_raw[:])
+        permute_columns(w_scale[:, 0:H], w1_scale_raw[:])
+        permute_columns(w1_code[:], w1_raw[:])
+
+        def first_layer(bank, code, row, t, j, lo, width):
+            cols = slice(t * P, (t + 1) * P)
+            nc.tensor.matmul_mx(
+                out=bank,
+                lhsT=code[:, cols].bitcast(FP8X4),
+                lhsT_scale=w_scale[:, row + t * P : row + (t + 1) * P],
+                rhs=x_code[j][:, lo : lo + width].bitcast(FP8X4),
+                rhs_scale=x_scale[X_ROW:P, j * CHUNK + lo : j * CHUNK + lo + width],
+                start=True,
+                stop=True,
+            )
+
+        def gated(dst, a_view, b_view, shape):
+            b_sb = ring.tile([P, CHUNK], F32, name="b_sb", align_bytes=64)
+            b_dst = b_sb[:] if shape is None else b_sb[:].rearrange("p (n u) -> p n u", u=2)
+            nc.scalar.activation(out=b_dst, in_=b_view, func=COPY)
+            nc.vector.scalar_tensor_tensor(
+                out=dst, in0=a_view, scalar=0.0, in1=b_dst, op0=ALU.max, op1=ALU.mult
+            )
+
+        for j in range(T // CHUNK):
+            for t in range(2):
+                b_bank = psum_b.tile([P, CHUNK], F32, name="b_bank")
+                a_bank = psum_a.tile([P, CHUNK], F32, name="a_bank")
+                first_layer(b_bank[:], w3_code, W3_ROW, 2 + t, j, 0, CHUNK)
+                first_layer(a_bank[:], w1_code, W1_ROW, 2 + t, j, 0, CHUNK)
+                gated(h_single[t][:, j * CHUNK : (j + 1) * CHUNK], a_bank[:], b_bank[:], None)
+            for half in range(2):
+                b_bank = psum_b.tile([P, CHUNK], F32, name="b_bank")
+                a_bank = psum_a.tile([P, CHUNK], F32, name="a_bank")
+                for t in range(2):
+                    first_layer(b_bank[:, t * HALF : (t + 1) * HALF], w3_code, W3_ROW, t, j, half * HALF, HALF)
+                for t in range(2):
+                    first_layer(a_bank[:, t * HALF : (t + 1) * HALF], w1_code, W1_ROW, t, j, half * HALF, HALF)
+                lo = 2 * (j * CHUNK + half * HALF)
+                gated(
+                    h_pair[:, lo : lo + 2 * HALF].rearrange("p (n u) -> p n u", u=2),
+                    a_bank[:].rearrange("p (u n) -> p n u", u=2),
+                    b_bank[:].rearrange("p (u n) -> p n u", u=2),
+                    2,
+                )
+
+        pairs = [keep.tile([P, 4 * C], BF16, name="pairs%d" % e, align_bytes=64) for e in range(E)]
+        quads = [keep.tile([P, 4 * C], BF16, name="quads%d" % e, align_bytes=64) for e in range(E)]
+        h_code = [keep.tile([P, C], U32, name="h_code%d" % e, align_bytes=64) for e in range(E)]
+        h_scale = [keep.tile([P, C], U8, name="h_scale%d" % e, align_bytes=64) for e in range(E)]
+        y_sb = [keep.tile([P, C], F32, name="y_sb%d" % e, align_bytes=64) for e in range(E)]
+
+        def slots(e):
+            return offsets[:, e * C // 16 : (e + 1) * C // 16]
+
+        def gather_vector(e):
+            nc.vector.tensor_copy(out=pairs[e][:, 0 : 2 * C].bitcast(U32), in_=h_pair[:].bitcast(U32).indirect(slots(e)))
+
+        def gather_scalar(e):
+            for t in range(2):
+                nc.scalar.activation(
+                    out=pairs[e][:, 2 * C + t : 4 * C : 2], in_=h_single[t][:].indirect(slots(e)), func=COPY
+                )
+
+        def interleave(e):
+            nc.scalar.copy(
+                out=quads[e][:].bitcast(U32).rearrange("p (n u) -> p n u", u=2),
+                in_=pairs[e][:].bitcast(U32).rearrange("p (u n) -> p n u", u=2),
+            )
+
+        def quantise(e):
+            nc.vector.quantize_mx(out=h_code[e][:].bitcast(FP8X4), scales=h_scale[e][:], in_=quads[e][:])
+
+        def second_layer(e):
+            y_bank = psum_y.tile([P, C], F32, name="y_bank")
+            nc.tensor.matmul_mx(
+                out=y_bank[:],
+                lhsT=w2_code[:, e * 2 * N : (e + 1) * 2 * N].bitcast(FP4X4),
+                lhsT_scale=w2_scale[:, e * N : (e + 1) * N],
+                rhs=h_code[e][:].bitcast(FP8X4),
+                rhs_scale=h_scale[e][:],
+                start=True,
+                stop=True,
+            )
+            nc.scalar.activation(out=y_sb[e][:], in_=y_bank[:], func=COPY)
+
+        def scatter(e):
+            nc.vector.tensor_tensor(
+                result[:].indirect(slots(e)), y_sb[e][:], gate_sb[:, e * C : (e + 1) * C], ALU.mult
+            )
+
+        for step in range(E + 3):
+            if step < E:
+                gather_vector(step)
+                gather_scalar(step)
+                interleave(step)
+            if 1 <= step < E + 1:
+                quantise(step - 1)
+                second_layer(step - 1)
+            if 3 <= step:
+                scatter(step - 3)
+
+        nc.sync.dma_start(out=out, in_=result[:])

@@ -22,6 +22,12 @@ HALF = 256
 X_ROW = 0
 W1_ROW = 0
 W3_ROW = H
+V_SLOTS = 4
+S_SLOTS = 2
+ORDER = (
+    "ga0 gb0 gv0 gv1 ga1 il0 gv2 gb1 gv3 qu0 ga2 il1 gv4 gb2 qu1 ev0 gv5 ga3 il2 gb3 sc0 ev1 qu2 ga4 il3 gb4 "
+    "sc1 ev2 qu3 ga5 il4 gb5 sc2 ev3 qu4 il5 sc3 ev4 qu5 sc4 ev5 sc5"
+)
 
 
 def tile_moe_sup_glu_relu_kernel(
@@ -30,10 +36,9 @@ def tile_moe_sup_glu_relu_kernel(
     nc = tc.nc
     with ExitStack() as ctx:
         keep = ctx.enter_context(tc.tile_pool(name="keep", bufs=1))
-        ring = ctx.enter_context(tc.tile_pool(name="ring", bufs=3))
-        psum_a = ctx.enter_context(tc.psum_pool(name="psum_a", bufs=3))
-        psum_b = ctx.enter_context(tc.psum_pool(name="psum_b", bufs=3))
-        psum_y = ctx.enter_context(tc.psum_pool(name="psum_y", bufs=2))
+        ring = ctx.enter_context(tc.tile_pool(name="ring", bufs=12))
+        psum_a = ctx.enter_context(tc.psum_pool(name="psum_a", bufs=4))
+        psum_b = ctx.enter_context(tc.psum_pool(name="psum_b", bufs=4))
 
         offsets = keep.tile([P, T // 16], U16, name="offsets")
         w1_scale_raw = keep.tile([P, H], U8, name="w1_scale_raw", align_bytes=64)
@@ -100,6 +105,18 @@ def tile_moe_sup_glu_relu_kernel(
         permute_columns(w_scale[:, 0:H], w1_scale_raw[:])
         permute_columns(w1_code[:], w1_raw[:])
 
+        warm_bank = psum_a.tile([P, CHUNK], F32, name="a_bank")
+        for width in (CHUNK, CHUNK, HALF):
+            nc.tensor.matmul_mx(
+                out=warm_bank[:, 0:width],
+                lhsT=w3_raw[:, 0:P].bitcast(FP8X4),
+                lhsT_scale=w3_scale_raw[:, 0:P],
+                rhs=w3_raw[:, 0:width].bitcast(FP8X4),
+                rhs_scale=w3_scale_raw[:, 0:width],
+                start=True,
+                stop=True,
+            )
+
         def first_layer(bank, code, row, t, j, lo, width):
             cols = slice(t * P, (t + 1) * P)
             nc.tensor.matmul_mx(
@@ -124,16 +141,16 @@ def tile_moe_sup_glu_relu_kernel(
             for t in range(2):
                 b_bank = psum_b.tile([P, CHUNK], F32, name="b_bank")
                 a_bank = psum_a.tile([P, CHUNK], F32, name="a_bank")
-                first_layer(b_bank[:], w3_code, W3_ROW, 2 + t, j, 0, CHUNK)
                 first_layer(a_bank[:], w1_code, W1_ROW, 2 + t, j, 0, CHUNK)
+                first_layer(b_bank[:], w3_code, W3_ROW, 2 + t, j, 0, CHUNK)
                 gated(h_single[t][:, j * CHUNK : (j + 1) * CHUNK], a_bank[:], b_bank[:], None)
             for half in range(2):
                 b_bank = psum_b.tile([P, CHUNK], F32, name="b_bank")
                 a_bank = psum_a.tile([P, CHUNK], F32, name="a_bank")
                 for t in range(2):
-                    first_layer(b_bank[:, t * HALF : (t + 1) * HALF], w3_code, W3_ROW, t, j, half * HALF, HALF)
-                for t in range(2):
                     first_layer(a_bank[:, t * HALF : (t + 1) * HALF], w1_code, W1_ROW, t, j, half * HALF, HALF)
+                for t in range(2):
+                    first_layer(b_bank[:, t * HALF : (t + 1) * HALF], w3_code, W3_ROW, t, j, half * HALF, HALF)
                 lo = 2 * (j * CHUNK + half * HALF)
                 gated(
                     h_pair[:, lo : lo + 2 * HALF].rearrange("p (n u) -> p n u", u=2),
@@ -142,7 +159,8 @@ def tile_moe_sup_glu_relu_kernel(
                     2,
                 )
 
-        pairs = [keep.tile([P, 4 * C], BF16, name="pairs%d" % e, align_bytes=64) for e in range(E)]
+        pairs = keep.tile([P, V_SLOTS + S_SLOTS, 2 * C], BF16, name="pairs", align_bytes=64)
+        y_banks = {}
         quads = [keep.tile([P, 4 * C], BF16, name="quads%d" % e, align_bytes=64) for e in range(E)]
         h_code = [keep.tile([P, C], U32, name="h_code%d" % e, align_bytes=64) for e in range(E)]
         h_scale = [keep.tile([P, C], U8, name="h_scale%d" % e, align_bytes=64) for e in range(E)]
@@ -152,25 +170,25 @@ def tile_moe_sup_glu_relu_kernel(
             return offsets[:, e * C // 16 : (e + 1) * C // 16]
 
         def gather_vector(e):
-            nc.vector.tensor_copy(out=pairs[e][:, 0 : 2 * C].bitcast(U32), in_=h_pair[:].bitcast(U32).indirect(slots(e)))
+            nc.vector.tensor_copy(out=pairs[:, e % V_SLOTS, :].bitcast(U32), in_=h_pair[:].bitcast(U32).indirect(slots(e)))
 
-        def gather_scalar(e):
-            for t in range(2):
-                nc.scalar.activation(
-                    out=pairs[e][:, 2 * C + t : 4 * C : 2], in_=h_single[t][:].indirect(slots(e)), func=COPY
-                )
+        def gather_scalar(e, t):
+            nc.scalar.activation(
+                out=pairs[:, V_SLOTS + e % S_SLOTS, t : 2 * C : 2], in_=h_single[t][:].indirect(slots(e)), func=COPY
+            )
 
         def interleave(e):
+            lo, hi = e % V_SLOTS, V_SLOTS + e % S_SLOTS
             nc.scalar.copy(
                 out=quads[e][:].bitcast(U32).rearrange("p (n u) -> p n u", u=2),
-                in_=pairs[e][:].bitcast(U32).rearrange("p (u n) -> p n u", u=2),
+                in_=pairs[:].bitcast(U32)[:, lo : hi + 1 : hi - lo, :].rearrange("p u n -> p n u"),
             )
 
         def quantise(e):
             nc.vector.quantize_mx(out=h_code[e][:].bitcast(FP8X4), scales=h_scale[e][:], in_=quads[e][:])
 
         def second_layer(e):
-            y_bank = psum_y.tile([P, C], F32, name="y_bank")
+            y_bank = psum_b.tile([P, C], F32, name="b_bank")
             nc.tensor.matmul_mx(
                 out=y_bank[:],
                 lhsT=w2_code[:, e * 2 * N : (e + 1) * 2 * N].bitcast(FP4X4),
@@ -180,22 +198,33 @@ def tile_moe_sup_glu_relu_kernel(
                 start=True,
                 stop=True,
             )
-            nc.scalar.activation(out=y_sb[e][:], in_=y_bank[:], func=COPY)
+            y_banks[e] = y_bank
+
+        def evacuate(e):
+            nc.scalar.activation(out=y_sb[e][:], in_=y_banks[e][:], func=COPY)
 
         def scatter(e):
             nc.vector.tensor_tensor(
                 result[:].indirect(slots(e)), y_sb[e][:], gate_sb[:, e * C : (e + 1) * C], ALU.mult
             )
 
-        for step in range(E + 3):
-            if step < E:
-                gather_vector(step)
-                gather_scalar(step)
-                interleave(step)
-            if 1 <= step < E + 1:
-                quantise(step - 1)
-                second_layer(step - 1)
-            if 3 <= step:
-                scatter(step - 3)
+        order = ORDER.split()
+        for item in order:
+            kind, e = item[:2], int(item[2])
+            if kind == "gv":
+                gather_vector(e)
+            elif kind == "ga":
+                gather_scalar(e, 0)
+            elif kind == "gb":
+                gather_scalar(e, 1)
+            elif kind == "il":
+                interleave(e)
+            elif kind == "qu":
+                quantise(e)
+                second_layer(e)
+            elif kind == "ev":
+                evacuate(e)
+            else:
+                scatter(e)
 
         nc.sync.dma_start(out=out, in_=result[:])

@@ -19,9 +19,6 @@ COPY = mybir.ActivationFunctionType.Copy
 P = 128
 CHUNK = 512
 HALF = 256
-X_ROW = 0
-W1_ROW = 0
-W3_ROW = H
 V_SLOTS = 4
 S_SLOTS = 2
 ORDER = (
@@ -41,10 +38,12 @@ def tile_moe_sup_glu_relu_kernel(
         psum_b = ctx.enter_context(tc.psum_pool(name="psum_b", bufs=4))
 
         offsets = keep.tile([P, T // 16], U16, name="offsets")
-        w1_scale_raw = keep.tile([P, H], U8, name="w1_scale_raw", align_bytes=64)
-        w3_scale_raw = keep.tile([P, H], U8, name="w3_scale_raw", align_bytes=64)
-        w_scale = keep.tile([P, 2 * H], U8, name="w_scale", align_bytes=64)
-        x_scale = keep.tile([P, T], U8, name="x_scale", align_bytes=64)
+        loaded_scales = keep.tile([P, 2 * H + T], U8, name="loaded_scales", align_bytes=64)
+        w1_scale_raw = loaded_scales[:, 0:H]
+        w3_scale_raw = loaded_scales[:, H : 2 * H]
+        x_scale = loaded_scales[:, 2 * H : 2 * H + T]
+        w1_scale = keep.tile([P, H], U8, name="w1_scale", align_bytes=64)
+        w3_scale = keep.tile([P, H], U8, name="w3_scale", align_bytes=64)
         w2_scale = keep.tile([P, E * N], U8, name="w2_scale", align_bytes=64)
         w1_raw = keep.tile([P, H], I32, name="w1_raw", align_bytes=64)
         w3_raw = keep.tile([P, H], I32, name="w3_raw", align_bytes=64)
@@ -56,8 +55,6 @@ def tile_moe_sup_glu_relu_kernel(
         h_pair = keep.tile([P, 2 * T], BF16, name="h_pair", align_bytes=64)
         h_single = [keep.tile([P, T], BF16, name="h_single%d" % t, align_bytes=64) for t in range(2)]
         result = keep.tile([P, T], F32, name="result", align_bytes=64)
-
-        nc.gpsimd.memset(w2_scale[:].bitcast(I32), 0)
 
         def load_scale_rows(engine, plane, scales, q):
             rows = scales[4 * q : 4 * q + 4, :].bitcast(I32)
@@ -71,19 +68,20 @@ def tile_moe_sup_glu_relu_kernel(
 
         xw = words(x_words[0])
         for q in range(4):
-            load_scale_rows(nc.scalar, w3_scale_raw, w3_scales[0], q)
-        for q in range(2):
-            load_scale_rows(nc.sync, x_scale, x_scales[0], q)
-        nc.sync.dma_start(out=w3_raw[:], in_=words(w3_words[0]))
-        nc.sync.dma_start(out=x_code[0][:], in_=xw[:, 0:CHUNK])
-        for q in range(2, 4):
-            load_scale_rows(nc.sync, x_scale, x_scales[0], q)
-        for q in range(4):
+            load_scale_rows(nc.scalar if q < 3 else nc.sync, w3_scale_raw, w3_scales[0], q)
+        for q in range(3):
             load_scale_rows(nc.sync, w1_scale_raw, w1_scales[0], q)
+        nc.sync.dma_start(out=w3_raw[:], in_=words(w3_words[0]))
         nc.sync.dma_start(out=w1_raw[:], in_=words(w1_words[0]))
+        load_scale_rows(nc.sync, w1_scale_raw, w1_scales[0], 3)
+        nc.sync.dma_start(out=x_code[0][:, 0:HALF], in_=xw[:, 0:HALF])
+        for q in range(4):
+            load_scale_rows(nc.sync if q < 2 else nc.scalar, x_scale, x_scales[0], q)
+        nc.sync.dma_start(out=x_code[0][:, HALF:CHUNK], in_=xw[:, HALF:CHUNK])
         for j in range(1, T // CHUNK):
             nc.sync.dma_start(out=x_code[j][:], in_=xw[:, j * CHUNK : (j + 1) * CHUNK])
         nc.sync.dma_start(offsets[:], offs)
+        nc.gpsimd.memset(w2_scale[:].bitcast(I32), 0)
         nc.sync.dma_start(
             out=w2_code[:].bitcast(I32).rearrange("p (e w) -> p e w", e=E),
             in_=w2_words.bitcast(I32).rearrange("e s p w -> p (e s) w"),
@@ -100,13 +98,18 @@ def tile_moe_sup_glu_relu_kernel(
                 out=dst.rearrange("p (t m) -> p m t", t=4), in_=src.rearrange("p (m t) -> p m t", t=4)
             )
 
-        permute_columns(w_scale[:, H : 2 * H], w3_scale_raw[:])
+        def permute_scales(dst, src):
+            nc.vector.tensor_copy(
+                out=dst.rearrange("p (t m) -> p t m", t=4), in_=src.rearrange("p (m t) -> p t m", t=4)
+            )
+
+        permute_scales(w3_scale[:], w3_scale_raw)
         permute_columns(w3_code[:], w3_raw[:])
-        permute_columns(w_scale[:, 0:H], w1_scale_raw[:])
+        permute_scales(w1_scale[:], w1_scale_raw)
         permute_columns(w1_code[:], w1_raw[:])
 
         warm_bank = psum_a.tile([P, CHUNK], F32, name="a_bank")
-        for width in (CHUNK, CHUNK, HALF):
+        for width in (CHUNK, CHUNK):
             nc.tensor.matmul_mx(
                 out=warm_bank[:, 0:width],
                 lhsT=w3_raw[:, 0:P].bitcast(FP8X4),
@@ -117,21 +120,21 @@ def tile_moe_sup_glu_relu_kernel(
                 stop=True,
             )
 
-        def first_layer(bank, code, row, t, j, lo, width):
+        def first_layer(bank, code, scale, t, j, lo, width):
             cols = slice(t * P, (t + 1) * P)
             nc.tensor.matmul_mx(
                 out=bank,
                 lhsT=code[:, cols].bitcast(FP8X4),
-                lhsT_scale=w_scale[:, row + t * P : row + (t + 1) * P],
+                lhsT_scale=scale[:, cols],
                 rhs=x_code[j][:, lo : lo + width].bitcast(FP8X4),
-                rhs_scale=x_scale[X_ROW:P, j * CHUNK + lo : j * CHUNK + lo + width],
+                rhs_scale=x_scale[:, j * CHUNK + lo : j * CHUNK + lo + width],
                 start=True,
                 stop=True,
             )
 
         def gated(dst, a_view, b_view, shape):
             b_sb = ring.tile([P, CHUNK], F32, name="b_sb", align_bytes=64)
-            b_dst = b_sb[:] if shape is None else b_sb[:].rearrange("p (n u) -> p n u", u=2)
+            b_dst = b_sb[:, 0:shape] if shape != 2 else b_sb[:].rearrange("p (n u) -> p n u", u=2)
             nc.scalar.activation(out=b_dst, in_=b_view, func=COPY)
             nc.vector.scalar_tensor_tensor(
                 out=dst, in0=a_view, scalar=0.0, in1=b_dst, op0=ALU.max, op1=ALU.mult
@@ -139,18 +142,23 @@ def tile_moe_sup_glu_relu_kernel(
 
         for j in range(T // CHUNK):
             for t in range(2):
-                b_bank = psum_b.tile([P, CHUNK], F32, name="b_bank")
-                a_bank = psum_a.tile([P, CHUNK], F32, name="a_bank")
-                first_layer(a_bank[:], w1_code, W1_ROW, 2 + t, j, 0, CHUNK)
-                first_layer(b_bank[:], w3_code, W3_ROW, 2 + t, j, 0, CHUNK)
-                gated(h_single[t][:, j * CHUNK : (j + 1) * CHUNK], a_bank[:], b_bank[:], None)
+                width = HALF if j == 0 and t == 0 else CHUNK
+                for lo in range(0, CHUNK, width):
+                    b_bank = psum_b.tile([P, width], F32, name="b_bank")
+                    a_bank = psum_a.tile([P, width], F32, name="a_bank")
+                    if width == HALF:
+                        first_layer(b_bank[:], w3_code, w3_scale, 2 + t, j, lo, width)
+                    first_layer(a_bank[:], w1_code, w1_scale, 2 + t, j, lo, width)
+                    if width == CHUNK:
+                        first_layer(b_bank[:], w3_code, w3_scale, 2 + t, j, lo, width)
+                    gated(h_single[t][:, j * CHUNK + lo : j * CHUNK + lo + width], a_bank[:], b_bank[:], width)
             for half in range(2):
                 b_bank = psum_b.tile([P, CHUNK], F32, name="b_bank")
                 a_bank = psum_a.tile([P, CHUNK], F32, name="a_bank")
                 for t in range(2):
-                    first_layer(a_bank[:, t * HALF : (t + 1) * HALF], w1_code, W1_ROW, t, j, half * HALF, HALF)
+                    first_layer(a_bank[:, t * HALF : (t + 1) * HALF], w1_code, w1_scale, t, j, half * HALF, HALF)
                 for t in range(2):
-                    first_layer(b_bank[:, t * HALF : (t + 1) * HALF], w3_code, W3_ROW, t, j, half * HALF, HALF)
+                    first_layer(b_bank[:, t * HALF : (t + 1) * HALF], w3_code, w3_scale, t, j, half * HALF, HALF)
                 lo = 2 * (j * CHUNK + half * HALF)
                 gated(
                     h_pair[:, lo : lo + 2 * HALF].rearrange("p (n u) -> p n u", u=2),

@@ -21,10 +21,7 @@ CHUNK = 512
 HALF = 256
 V_SLOTS = 4
 S_SLOTS = 2
-ORDER = (
-    "ga0 gb0 gv0 gv1 ga1 il0 gv2 gb1 gv3 qu0 ga2 il1 gv4 gb2 qu1 ev0 gv5 ga3 il2 gb3 sc0 ev1 qu2 ga4 il3 gb4 "
-    "sc1 ev2 qu3 ga5 il4 gb5 sc2 ev3 qu4 il5 sc3 ev4 qu5 sc4 ev5 sc5"
-)
+V_WEAVES = 0
 
 
 def tile_moe_sup_glu_relu_kernel(
@@ -38,10 +35,10 @@ def tile_moe_sup_glu_relu_kernel(
         psum_b = ctx.enter_context(tc.psum_pool(name="psum_b", bufs=4))
 
         offsets = keep.tile([P, T // 16], U16, name="offsets")
-        loaded_scales = keep.tile([P, 2 * H + T], U8, name="loaded_scales", align_bytes=64)
+        loaded_scales = keep.tile([P, 2 * H], U8, name="loaded_scales", align_bytes=64)
         w1_scale_raw = loaded_scales[:, 0:H]
         w3_scale_raw = loaded_scales[:, H : 2 * H]
-        x_scale = loaded_scales[:, 2 * H : 2 * H + T]
+        x_scale = keep.tile([P, T], U8, name="x_scale", align_bytes=64)
         w1_scale = keep.tile([P, H], U8, name="w1_scale", align_bytes=64)
         w3_scale = keep.tile([P, H], U8, name="w3_scale", align_bytes=64)
         w2_scale = keep.tile([P, E * N], U8, name="w2_scale", align_bytes=64)
@@ -67,17 +64,20 @@ def tile_moe_sup_glu_relu_kernel(
             return ap.rearrange("p n t -> p (n t)").bitcast(I32)
 
         xw = words(x_words[0])
+        nc.vector.memset(x_scale[:].bitcast(I32), 0)
         for q in range(4):
-            load_scale_rows(nc.scalar if q < 3 else nc.sync, w3_scale_raw, w3_scales[0], q)
-        for q in range(3):
-            load_scale_rows(nc.sync, w1_scale_raw, w1_scales[0], q)
+            load_scale_rows(nc.scalar if q % 2 else nc.sync, w3_scale_raw, w3_scales[0], q)
+        for q in range(2):
+            load_scale_rows(nc.scalar if q % 2 else nc.sync, w1_scale_raw, w1_scales[0], q)
         nc.sync.dma_start(out=w3_raw[:], in_=words(w3_words[0]))
         nc.sync.dma_start(out=w1_raw[:], in_=words(w1_words[0]))
-        load_scale_rows(nc.sync, w1_scale_raw, w1_scales[0], 3)
-        nc.sync.dma_start(out=x_code[0][:, 0:HALF], in_=xw[:, 0:HALF])
+        for q in range(2, 4):
+            load_scale_rows(nc.sync, w1_scale_raw, w1_scales[0], q)
+        nc.sync.dma_start(out=x_code[0][:], in_=xw[:, 0:CHUNK])
         for q in range(4):
-            load_scale_rows(nc.sync if q < 2 else nc.scalar, x_scale, x_scales[0], q)
-        nc.sync.dma_start(out=x_code[0][:, HALF:CHUNK], in_=xw[:, HALF:CHUNK])
+            nc.sync.dma_start(
+                out=x_scale[32 * q : 32 * q + 4, :].bitcast(I32), in_=x_scales[0][4 * q : 4 * q + 4, :].bitcast(I32)
+            )
         for j in range(1, T // CHUNK):
             nc.sync.dma_start(out=x_code[j][:], in_=xw[:, j * CHUNK : (j + 1) * CHUNK])
         nc.sync.dma_start(offsets[:], offs)
@@ -105,8 +105,8 @@ def tile_moe_sup_glu_relu_kernel(
 
         permute_scales(w3_scale[:], w3_scale_raw)
         permute_columns(w3_code[:], w3_raw[:])
-        permute_scales(w1_scale[:], w1_scale_raw)
         permute_columns(w1_code[:], w1_raw[:])
+        permute_scales(w1_scale[:], w1_scale_raw)
 
         warm_bank = psum_a.tile([P, CHUNK], F32, name="a_bank")
         for width in (CHUNK, CHUNK):
@@ -140,32 +140,38 @@ def tile_moe_sup_glu_relu_kernel(
                 out=dst, in0=a_view, scalar=0.0, in1=b_dst, op0=ALU.max, op1=ALU.mult
             )
 
-        for j in range(T // CHUNK):
+        def single_unit(j, t):
+            width = HALF if j == 0 and t == 0 else CHUNK
+            for lo in range(0, CHUNK, width):
+                b_bank = psum_b.tile([P, width], F32, name="b_bank")
+                a_bank = psum_a.tile([P, width], F32, name="a_bank")
+                if width == HALF:
+                    first_layer(b_bank[:], w3_code, w3_scale, 2 + t, j, lo, width)
+                first_layer(a_bank[:], w1_code, w1_scale, 2 + t, j, lo, width)
+                if width == CHUNK:
+                    first_layer(b_bank[:], w3_code, w3_scale, 2 + t, j, lo, width)
+                gated(h_single[t][:, j * CHUNK + lo : j * CHUNK + lo + width], a_bank[:], b_bank[:], width)
+
+        def pair_unit(j, half):
+            b_bank = psum_b.tile([P, CHUNK], F32, name="b_bank")
+            a_bank = psum_a.tile([P, CHUNK], F32, name="a_bank")
             for t in range(2):
-                width = HALF if j == 0 and t == 0 else CHUNK
-                for lo in range(0, CHUNK, width):
-                    b_bank = psum_b.tile([P, width], F32, name="b_bank")
-                    a_bank = psum_a.tile([P, width], F32, name="a_bank")
-                    if width == HALF:
-                        first_layer(b_bank[:], w3_code, w3_scale, 2 + t, j, lo, width)
-                    first_layer(a_bank[:], w1_code, w1_scale, 2 + t, j, lo, width)
-                    if width == CHUNK:
-                        first_layer(b_bank[:], w3_code, w3_scale, 2 + t, j, lo, width)
-                    gated(h_single[t][:, j * CHUNK + lo : j * CHUNK + lo + width], a_bank[:], b_bank[:], width)
-            for half in range(2):
-                b_bank = psum_b.tile([P, CHUNK], F32, name="b_bank")
-                a_bank = psum_a.tile([P, CHUNK], F32, name="a_bank")
-                for t in range(2):
-                    first_layer(a_bank[:, t * HALF : (t + 1) * HALF], w1_code, w1_scale, t, j, half * HALF, HALF)
-                for t in range(2):
-                    first_layer(b_bank[:, t * HALF : (t + 1) * HALF], w3_code, w3_scale, t, j, half * HALF, HALF)
-                lo = 2 * (j * CHUNK + half * HALF)
-                gated(
-                    h_pair[:, lo : lo + 2 * HALF].rearrange("p (n u) -> p n u", u=2),
-                    a_bank[:].rearrange("p (u n) -> p n u", u=2),
-                    b_bank[:].rearrange("p (u n) -> p n u", u=2),
-                    2,
-                )
+                first_layer(a_bank[:, t * HALF : (t + 1) * HALF], w1_code, w1_scale, t, j, half * HALF, HALF)
+            for t in range(2):
+                first_layer(b_bank[:, t * HALF : (t + 1) * HALF], w3_code, w3_scale, t, j, half * HALF, HALF)
+            lo = 2 * (j * CHUNK + half * HALF)
+            gated(
+                h_pair[:, lo : lo + 2 * HALF].rearrange("p (n u) -> p n u", u=2),
+                a_bank[:].rearrange("p (u n) -> p n u", u=2),
+                b_bank[:].rearrange("p (u n) -> p n u", u=2),
+                2,
+            )
+
+        for j in range(T // CHUNK):
+            single_unit(j, 0)
+            single_unit(j, 1)
+            pair_unit(j, 0)
+            pair_unit(j, 1)
 
         pairs = keep.tile([P, V_SLOTS + S_SLOTS, 2 * C], BF16, name="pairs", align_bytes=64)
         y_banks = {}
@@ -187,9 +193,11 @@ def tile_moe_sup_glu_relu_kernel(
 
         def interleave(e):
             lo, hi = e % V_SLOTS, V_SLOTS + e % S_SLOTS
-            nc.scalar.copy(
-                out=quads[e][:].bitcast(U32).rearrange("p (n u) -> p n u", u=2),
-                in_=pairs[:].bitcast(U32)[:, lo : hi + 1 : hi - lo, :].rearrange("p u n -> p n u"),
+            word = I32 if e < V_WEAVES else U32
+            copy = nc.vector.tensor_copy if e < V_WEAVES else nc.scalar.copy
+            copy(
+                out=quads[e][:].bitcast(word).rearrange("p (n u) -> p n u", u=2),
+                in_=pairs[:].bitcast(word)[:, lo : hi + 1 : hi - lo, :].rearrange("p u n -> p n u"),
             )
 
         def quantise(e):
@@ -216,23 +224,24 @@ def tile_moe_sup_glu_relu_kernel(
                 result[:].indirect(slots(e)), y_sb[e][:], gate_sb[:, e * C : (e + 1) * C], ALU.mult
             )
 
-        order = ORDER.split()
-        for item in order:
-            kind, e = item[:2], int(item[2])
-            if kind == "gv":
-                gather_vector(e)
-            elif kind == "ga":
-                gather_scalar(e, 0)
-            elif kind == "gb":
-                gather_scalar(e, 1)
-            elif kind == "il":
+        gather_scalar(0, 0)
+        gather_scalar(0, 1)
+        for e in range(V_SLOTS - 1):
+            gather_vector(e)
+        for e in range(E + 1):
+            if e + 1 < E:
+                gather_scalar(e + 1, 0)
+            if e < E:
                 interleave(e)
-            elif kind == "qu":
+            if e + V_SLOTS - 1 < E:
+                gather_vector(e + V_SLOTS - 1)
+            if e < E:
                 quantise(e)
                 second_layer(e)
-            elif kind == "ev":
-                evacuate(e)
-            else:
-                scatter(e)
+            if e > 0:
+                evacuate(e - 1)
+                scatter(e - 1)
+            if e + 1 < E:
+                gather_scalar(e + 1, 1)
 
         nc.sync.dma_start(out=out, in_=result[:])

@@ -65,15 +65,16 @@ def tile_moe_sup_glu_relu_kernel(
 
         xw = words(x_words[0])
         nc.vector.memset(x_scale[:].bitcast(I32), 0)
+        nc.vector.memset(w2_scale[:].bitcast(I32), 0)
         for q in range(4):
             load_scale_rows(nc.scalar if q % 2 else nc.sync, w3_scale_raw, w3_scales[0], q)
-        for q in range(2):
-            load_scale_rows(nc.scalar if q % 2 else nc.sync, w1_scale_raw, w1_scales[0], q)
+        load_scale_rows(nc.sync, w1_scale_raw, w1_scales[0], 0)
+        load_scale_rows(nc.gpsimd, w1_scale_raw, w1_scales[0], 1)
+        nc.sync.dma_start(out=x_code[0][:], in_=xw[:, 0:CHUNK])
         nc.sync.dma_start(out=w3_raw[:], in_=words(w3_words[0]))
         nc.sync.dma_start(out=w1_raw[:], in_=words(w1_words[0]))
         for q in range(2, 4):
             load_scale_rows(nc.sync, w1_scale_raw, w1_scales[0], q)
-        nc.sync.dma_start(out=x_code[0][:], in_=xw[:, 0:CHUNK])
         for q in range(4):
             nc.sync.dma_start(
                 out=x_scale[32 * q : 32 * q + 4, :].bitcast(I32), in_=x_scales[0][4 * q : 4 * q + 4, :].bitcast(I32)
@@ -81,7 +82,6 @@ def tile_moe_sup_glu_relu_kernel(
         for j in range(1, T // CHUNK):
             nc.sync.dma_start(out=x_code[j][:], in_=xw[:, j * CHUNK : (j + 1) * CHUNK])
         nc.sync.dma_start(offsets[:], offs)
-        nc.gpsimd.memset(w2_scale[:].bitcast(I32), 0)
         nc.sync.dma_start(
             out=w2_code[:].bitcast(I32).rearrange("p (e w) -> p e w", e=E),
             in_=w2_words.bitcast(I32).rearrange("e s p w -> p (e s) w"),
@@ -112,9 +112,9 @@ def tile_moe_sup_glu_relu_kernel(
         for width in (CHUNK, CHUNK):
             nc.tensor.matmul_mx(
                 out=warm_bank[:, 0:width],
-                lhsT=w3_raw[:, 0:P].bitcast(FP8X4),
+                lhsT=x_code[0][:, 0:P].bitcast(FP8X4),
                 lhsT_scale=w3_scale_raw[:, 0:P],
-                rhs=w3_raw[:, 0:width].bitcast(FP8X4),
+                rhs=x_code[0][:, 0:width].bitcast(FP8X4),
                 rhs_scale=w3_scale_raw[:, 0:width],
                 start=True,
                 stop=True,
@@ -140,17 +140,15 @@ def tile_moe_sup_glu_relu_kernel(
                 out=dst, in0=a_view, scalar=0.0, in1=b_dst, op0=ALU.max, op1=ALU.mult
             )
 
-        def single_unit(j, t):
-            width = HALF if j == 0 and t == 0 else CHUNK
-            for lo in range(0, CHUNK, width):
-                b_bank = psum_b.tile([P, width], F32, name="b_bank")
-                a_bank = psum_a.tile([P, width], F32, name="a_bank")
-                if width == HALF:
-                    first_layer(b_bank[:], w3_code, w3_scale, 2 + t, j, lo, width)
-                first_layer(a_bank[:], w1_code, w1_scale, 2 + t, j, lo, width)
-                if width == CHUNK:
-                    first_layer(b_bank[:], w3_code, w3_scale, 2 + t, j, lo, width)
-                gated(h_single[t][:, j * CHUNK + lo : j * CHUNK + lo + width], a_bank[:], b_bank[:], width)
+        def single_unit(j, t, lo=0, width=CHUNK):
+            b_bank = psum_b.tile([P, width], F32, name="b_bank")
+            a_bank = psum_a.tile([P, width], F32, name="a_bank")
+            if width == HALF:
+                first_layer(b_bank[:], w3_code, w3_scale, 2 + t, j, lo, width)
+            first_layer(a_bank[:], w1_code, w1_scale, 2 + t, j, lo, width)
+            if width == CHUNK:
+                first_layer(b_bank[:], w3_code, w3_scale, 2 + t, j, lo, width)
+            gated(h_single[t][:, j * CHUNK + lo : j * CHUNK + lo + width], a_bank[:], b_bank[:], width)
 
         def pair_unit(j, half):
             b_bank = psum_b.tile([P, CHUNK], F32, name="b_bank")
@@ -167,7 +165,12 @@ def tile_moe_sup_glu_relu_kernel(
                 2,
             )
 
-        for j in range(T // CHUNK):
+        single_unit(0, 0, 0, HALF)
+        single_unit(0, 0, HALF, HALF)
+        single_unit(0, 1)
+        pair_unit(0, 0)
+        pair_unit(0, 1)
+        for j in range(1, T // CHUNK):
             single_unit(j, 0)
             single_unit(j, 1)
             pair_unit(j, 0)

@@ -70,7 +70,7 @@ def tile_moe_sup_glu_relu_kernel(
             load_scale_rows(nc.scalar if q % 2 else nc.sync, w3_scale_raw, w3_scales[0], q)
         load_scale_rows(nc.sync, w1_scale_raw, w1_scales[0], 0)
         load_scale_rows(nc.gpsimd, w1_scale_raw, w1_scales[0], 1)
-        nc.sync.dma_start(out=x_code[0][:], in_=xw[:, 0:CHUNK])
+        nc.sync.dma_start(out=x_code[0][:, 0:HALF], in_=xw[:, 0:HALF])
         nc.sync.dma_start(out=w3_raw[:], in_=words(w3_words[0]))
         nc.sync.dma_start(out=w1_raw[:], in_=words(w1_words[0]))
         for q in range(2, 4):
@@ -79,6 +79,7 @@ def tile_moe_sup_glu_relu_kernel(
             nc.sync.dma_start(
                 out=x_scale[32 * q : 32 * q + 4, :].bitcast(I32), in_=x_scales[0][4 * q : 4 * q + 4, :].bitcast(I32)
             )
+        nc.sync.dma_start(out=x_code[0][:, HALF:CHUNK], in_=xw[:, HALF:CHUNK])
         for j in range(1, T // CHUNK):
             nc.sync.dma_start(out=x_code[j][:], in_=xw[:, j * CHUNK : (j + 1) * CHUNK])
         nc.sync.dma_start(offsets[:], offs)
@@ -109,7 +110,7 @@ def tile_moe_sup_glu_relu_kernel(
         permute_scales(w1_scale[:], w1_scale_raw)
 
         warm_bank = psum_a.tile([P, CHUNK], F32, name="a_bank")
-        for width in (CHUNK, CHUNK):
+        for width in (HALF, HALF, HALF, HALF):
             nc.tensor.matmul_mx(
                 out=warm_bank[:, 0:width],
                 lhsT=x_code[0][:, 0:P].bitcast(FP8X4),

@@ -110,7 +110,7 @@ def tile_moe_sup_glu_relu_kernel(
         permute_scales(w1_scale[:], w1_scale_raw)
 
         warm_bank = psum_a.tile([P, CHUNK], F32, name="a_bank")
-        for width in (HALF, HALF, HALF, HALF):
+        for width in (HALF, HALF, HALF, HALF, HALF):
             nc.tensor.matmul_mx(
                 out=warm_bank[:, 0:width],
                 lhsT=x_code[0][:, 0:P].bitcast(FP8X4),

@@ -17,11 +17,14 @@ ALU = mybir.AluOpType
 COPY = mybir.ActivationFunctionType.Copy
 
 P = 128
+PACK = 4
+QUADRANTS = 4
 CHUNK = 512
-HALF = 256
-V_SLOTS = 4
-S_SLOTS = 2
-V_WEAVES = 0
+HALF = CHUNK // 2
+W3_COPIES = 12
+BANKS = 4
+VECTOR_AREAS = 4
+SCALAR_AREAS = 2
 
 
 def tile_moe_sup_glu_relu_kernel(
@@ -30,9 +33,9 @@ def tile_moe_sup_glu_relu_kernel(
     nc = tc.nc
     with ExitStack() as ctx:
         keep = ctx.enter_context(tc.tile_pool(name="keep", bufs=1))
-        ring = ctx.enter_context(tc.tile_pool(name="ring", bufs=12))
-        psum_a = ctx.enter_context(tc.psum_pool(name="psum_a", bufs=4))
-        psum_b = ctx.enter_context(tc.psum_pool(name="psum_b", bufs=4))
+        ring = ctx.enter_context(tc.tile_pool(name="ring", bufs=W3_COPIES))
+        psum_a = ctx.enter_context(tc.psum_pool(name="psum_a", bufs=BANKS))
+        psum_b = ctx.enter_context(tc.psum_pool(name="psum_b", bufs=BANKS))
 
         offsets = keep.tile([P, T // 16], U16, name="offsets")
         loaded_scales = keep.tile([P, 2 * H], U8, name="loaded_scales", align_bytes=64)
@@ -50,79 +53,82 @@ def tile_moe_sup_glu_relu_kernel(
         w2_code = keep.tile([P, E * 2 * N], U8, name="w2_code", align_bytes=64)
         gate_sb = keep.tile([P, T], F32, name="gate_sb", align_bytes=64)
         h_pair = keep.tile([P, 2 * T], BF16, name="h_pair", align_bytes=64)
-        h_single = [keep.tile([P, T], BF16, name="h_single%d" % t, align_bytes=64) for t in range(2)]
+        h_single = [keep.tile([P, T], BF16, name="h_single%d" % s, align_bytes=64) for s in range(2)]
         result = keep.tile([P, T], F32, name="result", align_bytes=64)
 
-        def load_scale_rows(engine, plane, scales, q):
+        def load_weight_scales(queue, tile_view, scales, q):
             rows = scales[4 * q : 4 * q + 4, :].bitcast(I32)
-            engine.dma_start(
-                out=plane[32 * q : 32 * q + 32, :].bitcast(I32),
+            queue.dma_start(
+                out=tile_view[32 * q : 32 * q + 32, :].bitcast(I32),
                 in_=rows.unsqueeze(0).to_broadcast([8, 4, rows.shape[1]]),
             )
 
         def words(ap):
-            return ap.rearrange("p n t -> p (n t)").bitcast(I32)
+            return ap.rearrange("p n d -> p (n d)").bitcast(I32)
 
         xw = words(x_words[0])
         nc.vector.memset(x_scale[:].bitcast(I32), 0)
         nc.vector.memset(w2_scale[:].bitcast(I32), 0)
-        for q in range(4):
-            load_scale_rows(nc.scalar if q % 2 else nc.sync, w3_scale_raw, w3_scales[0], q)
-        load_scale_rows(nc.sync, w1_scale_raw, w1_scales[0], 0)
-        load_scale_rows(nc.gpsimd, w1_scale_raw, w1_scales[0], 1)
+
+        for q in range(QUADRANTS):
+            load_weight_scales(nc.scalar if q % 2 else nc.sync, w3_scale_raw, w3_scales[0], q)
+        load_weight_scales(nc.sync, w1_scale_raw, w1_scales[0], 0)
+        load_weight_scales(nc.gpsimd, w1_scale_raw, w1_scales[0], 1)
         nc.sync.dma_start(out=x_code[0][:, 0:HALF], in_=xw[:, 0:HALF])
         nc.sync.dma_start(out=w3_raw[:], in_=words(w3_words[0]))
         nc.sync.dma_start(out=w1_raw[:], in_=words(w1_words[0]))
-        for q in range(2, 4):
-            load_scale_rows(nc.sync, w1_scale_raw, w1_scales[0], q)
-        for q in range(4):
+        for q in range(2, QUADRANTS):
+            load_weight_scales(nc.sync, w1_scale_raw, w1_scales[0], q)
+        for q in range(QUADRANTS):
             nc.sync.dma_start(
                 out=x_scale[32 * q : 32 * q + 4, :].bitcast(I32), in_=x_scales[0][4 * q : 4 * q + 4, :].bitcast(I32)
             )
         nc.sync.dma_start(out=x_code[0][:, HALF:CHUNK], in_=xw[:, HALF:CHUNK])
         for j in range(1, T // CHUNK):
             nc.sync.dma_start(out=x_code[j][:], in_=xw[:, j * CHUNK : (j + 1) * CHUNK])
+
         nc.sync.dma_start(offsets[:], offs)
         nc.sync.dma_start(
             out=w2_code[:].bitcast(I32).rearrange("p (e w) -> p e w", e=E),
             in_=w2_words.bitcast(I32).rearrange("e s p w -> p (e s) w"),
         )
-        for q in range(4):
-            nc.sync.dma_start(
+        for q in range(QUADRANTS):
+            queue = nc.gpsimd if q == QUADRANTS - 1 else nc.sync
+            queue.dma_start(
                 out=w2_scale[32 * q : 32 * q + 4, :].bitcast(I32).rearrange("r (e w) -> r e w", e=E),
                 in_=w2_scales.bitcast(I32)[:, 0, 4 * q : 4 * q + 4, :].rearrange("e r w -> r e w"),
             )
         nc.sync.dma_start(out=gate_sb[:], in_=gate)
 
-        def permute_columns(dst, src):
+        def reorder_words(dst, src):
             nc.vector.tensor_copy(
-                out=dst.rearrange("p (t m) -> p m t", t=4), in_=src.rearrange("p (m t) -> p m t", t=4)
+                out=dst.rearrange("p (d m) -> p m d", d=PACK), in_=src.rearrange("p (m d) -> p m d", d=PACK)
             )
 
-        def permute_scales(dst, src):
+        def reorder_scales(dst, src):
             nc.vector.tensor_copy(
-                out=dst.rearrange("p (t m) -> p t m", t=4), in_=src.rearrange("p (m t) -> p t m", t=4)
+                out=dst.rearrange("p (d m) -> p d m", d=PACK), in_=src.rearrange("p (m d) -> p d m", d=PACK)
             )
 
-        permute_scales(w3_scale[:], w3_scale_raw)
-        permute_columns(w3_code[:], w3_raw[:])
-        permute_columns(w1_code[:], w1_raw[:])
-        permute_scales(w1_scale[:], w1_scale_raw)
+        reorder_scales(w3_scale[:], w3_scale_raw)
+        reorder_words(w3_code[:], w3_raw[:])
+        reorder_words(w1_code[:], w1_raw[:])
+        reorder_scales(w1_scale[:], w1_scale_raw)
 
         warm_bank = psum_a.tile([P, CHUNK], F32, name="a_bank")
-        for width in (HALF, HALF, HALF, HALF, HALF):
+        for moving, width in ((x_code[0], HALF), (x_code[0], HALF), (x_code[0], HALF), (w3_raw, CHUNK)):
             nc.tensor.matmul_mx(
                 out=warm_bank[:, 0:width],
                 lhsT=x_code[0][:, 0:P].bitcast(FP8X4),
                 lhsT_scale=w3_scale_raw[:, 0:P],
-                rhs=x_code[0][:, 0:width].bitcast(FP8X4),
+                rhs=moving[:, 0:width].bitcast(FP8X4),
                 rhs_scale=w3_scale_raw[:, 0:width],
                 start=True,
                 stop=True,
             )
 
-        def first_layer(bank, code, scale, t, j, lo, width):
-            cols = slice(t * P, (t + 1) * P)
+        def first_layer(bank, code, scale, d, j, lo, width):
+            cols = slice(d * P, (d + 1) * P)
             nc.tensor.matmul_mx(
                 out=bank,
                 lhsT=code[:, cols].bitcast(FP8X4),
@@ -133,53 +139,47 @@ def tile_moe_sup_glu_relu_kernel(
                 stop=True,
             )
 
-        def gated(dst, a_view, b_view, shape):
-            b_sb = ring.tile([P, CHUNK], F32, name="b_sb", align_bytes=64)
-            b_dst = b_sb[:, 0:shape] if shape != 2 else b_sb[:].rearrange("p (n u) -> p n u", u=2)
-            nc.scalar.activation(out=b_dst, in_=b_view, func=COPY)
-            nc.vector.scalar_tensor_tensor(
-                out=dst, in0=a_view, scalar=0.0, in1=b_dst, op0=ALU.max, op1=ALU.mult
-            )
+        def gated(dst, a_view, b_view, b_sb):
+            nc.scalar.activation(out=b_sb, in_=b_view, func=COPY)
+            nc.vector.scalar_tensor_tensor(out=dst, in0=a_view, scalar=0.0, in1=b_sb, op0=ALU.max, op1=ALU.mult)
 
-        def single_unit(j, t, lo=0, width=CHUNK):
+        def single_plane(j, s, lo, width, w3_first):
             b_bank = psum_b.tile([P, width], F32, name="b_bank")
             a_bank = psum_a.tile([P, width], F32, name="a_bank")
-            if width == HALF:
-                first_layer(b_bank[:], w3_code, w3_scale, 2 + t, j, lo, width)
-            first_layer(a_bank[:], w1_code, w1_scale, 2 + t, j, lo, width)
-            if width == CHUNK:
-                first_layer(b_bank[:], w3_code, w3_scale, 2 + t, j, lo, width)
-            gated(h_single[t][:, j * CHUNK + lo : j * CHUNK + lo + width], a_bank[:], b_bank[:], width)
+            passes = [(a_bank, w1_code, w1_scale), (b_bank, w3_code, w3_scale)]
+            for bank, code, scale in reversed(passes) if w3_first else passes:
+                first_layer(bank[:], code, scale, 2 + s, j, lo, width)
+            b_sb = ring.tile([P, CHUNK], F32, name="b_sb", align_bytes=64)
+            gated(h_single[s][:, j * CHUNK + lo : j * CHUNK + lo + width], a_bank[:], b_bank[:], b_sb[:, 0:width])
 
-        def pair_unit(j, half):
+        def pair_planes(j, lo):
             b_bank = psum_b.tile([P, CHUNK], F32, name="b_bank")
             a_bank = psum_a.tile([P, CHUNK], F32, name="a_bank")
-            for t in range(2):
-                first_layer(a_bank[:, t * HALF : (t + 1) * HALF], w1_code, w1_scale, t, j, half * HALF, HALF)
-            for t in range(2):
-                first_layer(b_bank[:, t * HALF : (t + 1) * HALF], w3_code, w3_scale, t, j, half * HALF, HALF)
-            lo = 2 * (j * CHUNK + half * HALF)
+            for bank, code, scale in ((a_bank, w1_code, w1_scale), (b_bank, w3_code, w3_scale)):
+                for d in range(2):
+                    first_layer(bank[:, d * HALF : (d + 1) * HALF], code, scale, d, j, lo, HALF)
+            b_sb = ring.tile([P, CHUNK], F32, name="b_sb", align_bytes=64)
+            first = 2 * (j * CHUNK + lo)
             gated(
-                h_pair[:, lo : lo + 2 * HALF].rearrange("p (n u) -> p n u", u=2),
-                a_bank[:].rearrange("p (u n) -> p n u", u=2),
-                b_bank[:].rearrange("p (u n) -> p n u", u=2),
-                2,
+                h_pair[:, first : first + 2 * HALF].rearrange("p (n d) -> p n d", d=2),
+                a_bank[:].rearrange("p (d n) -> p n d", d=2),
+                b_bank[:].rearrange("p (d n) -> p n d", d=2),
+                b_sb[:].rearrange("p (n d) -> p n d", d=2),
             )
 
-        single_unit(0, 0, 0, HALF)
-        single_unit(0, 0, HALF, HALF)
-        single_unit(0, 1)
-        pair_unit(0, 0)
-        pair_unit(0, 1)
-        for j in range(1, T // CHUNK):
-            single_unit(j, 0)
-            single_unit(j, 1)
-            pair_unit(j, 0)
-            pair_unit(j, 1)
+        for j in range(T // CHUNK):
+            if j == 0:
+                single_plane(j, 0, 0, HALF, True)
+                single_plane(j, 0, HALF, HALF, True)
+            else:
+                single_plane(j, 0, 0, CHUNK, False)
+            single_plane(j, 1, 0, CHUNK, False)
+            pair_planes(j, 0)
+            pair_planes(j, HALF)
 
-        pairs = keep.tile([P, V_SLOTS + S_SLOTS, 2 * C], BF16, name="pairs", align_bytes=64)
+        areas = keep.tile([P, VECTOR_AREAS + SCALAR_AREAS, 2 * C], BF16, name="areas", align_bytes=64)
         y_banks = {}
-        quads = [keep.tile([P, 4 * C], BF16, name="quads%d" % e, align_bytes=64) for e in range(E)]
+        quads = [keep.tile([P, PACK * C], BF16, name="quads%d" % e, align_bytes=64) for e in range(E)]
         h_code = [keep.tile([P, C], U32, name="h_code%d" % e, align_bytes=64) for e in range(E)]
         h_scale = [keep.tile([P, C], U8, name="h_scale%d" % e, align_bytes=64) for e in range(E)]
         y_sb = [keep.tile([P, C], F32, name="y_sb%d" % e, align_bytes=64) for e in range(E)]
@@ -187,21 +187,23 @@ def tile_moe_sup_glu_relu_kernel(
         def slots(e):
             return offsets[:, e * C // 16 : (e + 1) * C // 16]
 
-        def gather_vector(e):
-            nc.vector.tensor_copy(out=pairs[:, e % V_SLOTS, :].bitcast(U32), in_=h_pair[:].bitcast(U32).indirect(slots(e)))
+        def gather_pairs(e):
+            nc.vector.tensor_copy(
+                out=areas[:, e % VECTOR_AREAS, :].bitcast(U32), in_=h_pair[:].bitcast(U32).indirect(slots(e))
+            )
 
-        def gather_scalar(e, t):
+        def gather_single(e, s):
             nc.scalar.activation(
-                out=pairs[:, V_SLOTS + e % S_SLOTS, t : 2 * C : 2], in_=h_single[t][:].indirect(slots(e)), func=COPY
+                out=areas[:, VECTOR_AREAS + e % SCALAR_AREAS, s : 2 * C : 2],
+                in_=h_single[s][:].indirect(slots(e)),
+                func=COPY,
             )
 
         def interleave(e):
-            lo, hi = e % V_SLOTS, V_SLOTS + e % S_SLOTS
-            word = I32 if e < V_WEAVES else U32
-            copy = nc.vector.tensor_copy if e < V_WEAVES else nc.scalar.copy
-            copy(
-                out=quads[e][:].bitcast(word).rearrange("p (n u) -> p n u", u=2),
-                in_=pairs[:].bitcast(word)[:, lo : hi + 1 : hi - lo, :].rearrange("p u n -> p n u"),
+            lo, hi = e % VECTOR_AREAS, VECTOR_AREAS + e % SCALAR_AREAS
+            nc.scalar.copy(
+                out=quads[e][:].bitcast(U32).rearrange("p (u half) -> p u half", half=2),
+                in_=areas[:].bitcast(U32)[:, lo : hi + 1 : hi - lo, :].rearrange("p half u -> p u half"),
             )
 
         def quantise(e):
@@ -228,17 +230,17 @@ def tile_moe_sup_glu_relu_kernel(
                 result[:].indirect(slots(e)), y_sb[e][:], gate_sb[:, e * C : (e + 1) * C], ALU.mult
             )
 
-        gather_scalar(0, 0)
-        gather_scalar(0, 1)
-        for e in range(V_SLOTS - 1):
-            gather_vector(e)
+        gather_single(0, 0)
+        gather_single(0, 1)
+        for e in range(VECTOR_AREAS - 1):
+            gather_pairs(e)
         for e in range(E + 1):
             if e + 1 < E:
-                gather_scalar(e + 1, 0)
+                gather_single(e + 1, 0)
             if e < E:
                 interleave(e)
-            if e + V_SLOTS - 1 < E:
-                gather_vector(e + V_SLOTS - 1)
+            if e + VECTOR_AREAS - 1 < E:
+                gather_pairs(e + VECTOR_AREAS - 1)
             if e < E:
                 quantise(e)
                 second_layer(e)
@@ -246,6 +248,6 @@ def tile_moe_sup_glu_relu_kernel(
                 evacuate(e - 1)
                 scatter(e - 1)
             if e + 1 < E:
-                gather_scalar(e + 1, 1)
+                gather_single(e + 1, 1)
 
         nc.sync.dma_start(out=out, in_=result[:])

@@ -23,7 +23,8 @@ CHUNK = 512
 HALF = CHUNK // 2
 W3_COPIES = 12
 BANKS = 4
-VECTOR_AREAS = 4
+VECTOR_AREAS = 5
+AREA = (3, 0, 1, 2, 3, 4)
 SCALAR_AREAS = 2
 
 
@@ -143,11 +144,10 @@ def tile_moe_sup_glu_relu_kernel(
             nc.scalar.activation(out=b_sb, in_=b_view, func=COPY)
             nc.vector.scalar_tensor_tensor(out=dst, in0=a_view, scalar=0.0, in1=b_sb, op0=ALU.max, op1=ALU.mult)
 
-        def single_plane(j, s, lo, width, w3_first):
+        def single_plane(j, s, lo, width):
             b_bank = psum_b.tile([P, width], F32, name="b_bank")
             a_bank = psum_a.tile([P, width], F32, name="a_bank")
-            passes = [(a_bank, w1_code, w1_scale), (b_bank, w3_code, w3_scale)]
-            for bank, code, scale in reversed(passes) if w3_first else passes:
+            for bank, code, scale in ((b_bank, w3_code, w3_scale), (a_bank, w1_code, w1_scale)):
                 first_layer(bank[:], code, scale, 2 + s, j, lo, width)
             b_sb = ring.tile([P, CHUNK], F32, name="b_sb", align_bytes=64)
             gated(h_single[s][:, j * CHUNK + lo : j * CHUNK + lo + width], a_bank[:], b_bank[:], b_sb[:, 0:width])
@@ -155,7 +155,7 @@ def tile_moe_sup_glu_relu_kernel(
         def pair_planes(j, lo):
             b_bank = psum_b.tile([P, CHUNK], F32, name="b_bank")
             a_bank = psum_a.tile([P, CHUNK], F32, name="a_bank")
-            for bank, code, scale in ((a_bank, w1_code, w1_scale), (b_bank, w3_code, w3_scale)):
+            for bank, code, scale in ((b_bank, w3_code, w3_scale), (a_bank, w1_code, w1_scale)):
                 for d in range(2):
                     first_layer(bank[:, d * HALF : (d + 1) * HALF], code, scale, d, j, lo, HALF)
             b_sb = ring.tile([P, CHUNK], F32, name="b_sb", align_bytes=64)
@@ -169,11 +169,11 @@ def tile_moe_sup_glu_relu_kernel(
 
         for j in range(T // CHUNK):
             if j == 0:
-                single_plane(j, 0, 0, HALF, True)
-                single_plane(j, 0, HALF, HALF, True)
+                single_plane(j, 0, 0, HALF)
+                single_plane(j, 0, HALF, HALF)
             else:
-                single_plane(j, 0, 0, CHUNK, False)
-            single_plane(j, 1, 0, CHUNK, False)
+                single_plane(j, 0, 0, CHUNK)
+            single_plane(j, 1, 0, CHUNK)
             pair_planes(j, 0)
             pair_planes(j, HALF)
 
@@ -184,12 +184,13 @@ def tile_moe_sup_glu_relu_kernel(
         h_scale = [keep.tile([P, C], U8, name="h_scale%d" % e, align_bytes=64) for e in range(E)]
         y_sb = [keep.tile([P, C], F32, name="y_sb%d" % e, align_bytes=64) for e in range(E)]
 
-        def slots(e):
-            return offsets[:, e * C // 16 : (e + 1) * C // 16]
+        def slots(e, count=1):
+            return offsets[:, e * C // 16 : (e + count) * C // 16]
 
-        def gather_pairs(e):
+        def gather_pairs(e, count):
             nc.vector.tensor_copy(
-                out=areas[:, e % VECTOR_AREAS, :].bitcast(U32), in_=h_pair[:].bitcast(U32).indirect(slots(e))
+                out=areas[:, AREA[e] : AREA[e] + count, :].rearrange("p a w -> p (a w)").bitcast(U32),
+                in_=h_pair[:].bitcast(U32).indirect(slots(e, count)),
             )
 
         def gather_single(e, s):
@@ -200,7 +201,7 @@ def tile_moe_sup_glu_relu_kernel(
             )
 
         def interleave(e):
-            lo, hi = e % VECTOR_AREAS, VECTOR_AREAS + e % SCALAR_AREAS
+            lo, hi = AREA[e], VECTOR_AREAS + e % SCALAR_AREAS
             nc.scalar.copy(
                 out=quads[e][:].bitcast(U32).rearrange("p (u half) -> p u half", half=2),
                 in_=areas[:].bitcast(U32)[:, lo : hi + 1 : hi - lo, :].rearrange("p half u -> p u half"),
@@ -232,18 +233,19 @@ def tile_moe_sup_glu_relu_kernel(
 
         gather_single(0, 0)
         gather_single(0, 1)
-        for e in range(VECTOR_AREAS - 1):
-            gather_pairs(e)
+        gather_pairs(0, 1)
+        gather_pairs(1, 1)
+        gather_pairs(2, 2)
         for e in range(E + 1):
             if e + 1 < E:
                 gather_single(e + 1, 0)
             if e < E:
                 interleave(e)
-            if e + VECTOR_AREAS - 1 < E:
-                gather_pairs(e + VECTOR_AREAS - 1)
             if e < E:
                 quantise(e)
                 second_layer(e)
+            if e == 0:
+                gather_pairs(4, 2)
             if e > 0:
                 evacuate(e - 1)
                 scatter(e - 1)

@@ -22,10 +22,12 @@ QUADRANTS = 4
 CHUNK = 512
 HALF = CHUNK // 2
 W3_COPIES = 12
+QUAD_AREA = (7, 15, 2, 4, 17, 19)
+GATE_AREA = 9
+LOW_AREA = (0, 1, 0, 1, QUAD_AREA[2], QUAD_AREA[3])
+HIGH_AREA = (6, 6, QUAD_AREA[0], GATE_AREA + 1, GATE_AREA + 2, GATE_AREA + 3)
+AREAS = 21
 BANKS = 4
-VECTOR_AREAS = 5
-AREA = (3, 0, 1, 2, 3, 4)
-SCALAR_AREAS = 2
 
 
 def tile_moe_sup_glu_relu_kernel(
@@ -52,9 +54,10 @@ def tile_moe_sup_glu_relu_kernel(
         w3_code = keep.tile([P, H], I32, name="w3_code", align_bytes=64)
         x_code = [keep.tile([P, CHUNK], I32, name="x_code%d" % j, align_bytes=64) for j in range(T // CHUNK)]
         w2_code = keep.tile([P, E * 2 * N], U8, name="w2_code", align_bytes=64)
-        gate_sb = keep.tile([P, T], F32, name="gate_sb", align_bytes=64)
-        h_pair = keep.tile([P, 2 * T], BF16, name="h_pair", align_bytes=64)
-        h_single = [keep.tile([P, T], BF16, name="h_single%d" % s, align_bytes=64) for s in range(2)]
+        areas = keep.tile([P, AREAS * C], U32, name="areas", align_bytes=64)
+        gate_sb = areas[:, GATE_AREA * C : (GATE_AREA + E) * C].bitcast(F32)
+        h_pair = [keep.tile([P, 2 * T], BF16, name="h_pair%d" % s, align_bytes=64) for s in range(2)]
+        h_single = keep.tile([P, 2 * T], BF16, name="h_single", align_bytes=64)
         result = keep.tile([P, T], F32, name="result", align_bytes=64)
 
         def load_weight_scales(queue, tile_view, scales, q):
@@ -99,7 +102,7 @@ def tile_moe_sup_glu_relu_kernel(
                 out=w2_scale[32 * q : 32 * q + 4, :].bitcast(I32).rearrange("r (e w) -> r e w", e=E),
                 in_=w2_scales.bitcast(I32)[:, 0, 4 * q : 4 * q + 4, :].rearrange("e r w -> r e w"),
             )
-        nc.sync.dma_start(out=gate_sb[:], in_=gate)
+        nc.sync.dma_start(out=gate_sb, in_=gate)
 
         def reorder_words(dst, src):
             nc.vector.tensor_copy(
@@ -128,128 +131,135 @@ def tile_moe_sup_glu_relu_kernel(
                 stop=True,
             )
 
-        def first_layer(bank, code, scale, d, j, lo, width):
+        def first_layer(bank, code, scale, d, lo, width):
             cols = slice(d * P, (d + 1) * P)
             nc.tensor.matmul_mx(
                 out=bank,
                 lhsT=code[:, cols].bitcast(FP8X4),
                 lhsT_scale=scale[:, cols],
-                rhs=x_code[j][:, lo : lo + width].bitcast(FP8X4),
-                rhs_scale=x_scale[:, j * CHUNK + lo : j * CHUNK + lo + width],
+                rhs=x_code[lo // CHUNK][:, lo % CHUNK : lo % CHUNK + width].bitcast(FP8X4),
+                rhs_scale=x_scale[:, lo : lo + width],
                 start=True,
                 stop=True,
             )
 
-        def gated(dst, a_view, b_view, b_sb):
+        def gated_product(dst, a_view, b_view, b_sb):
             nc.scalar.activation(out=b_sb, in_=b_view, func=COPY)
             nc.vector.scalar_tensor_tensor(out=dst, in0=a_view, scalar=0.0, in1=b_sb, op0=ALU.max, op1=ALU.mult)
 
-        def single_plane(j, s, lo, width):
+        def single_plane(s, lo, width):
             b_bank = psum_b.tile([P, width], F32, name="b_bank")
             a_bank = psum_a.tile([P, width], F32, name="a_bank")
             for bank, code, scale in ((b_bank, w3_code, w3_scale), (a_bank, w1_code, w1_scale)):
-                first_layer(bank[:], code, scale, 2 + s, j, lo, width)
+                first_layer(bank[:], code, scale, 2 + s, lo, width)
             b_sb = ring.tile([P, CHUNK], F32, name="b_sb", align_bytes=64)
-            gated(h_single[s][:, j * CHUNK + lo : j * CHUNK + lo + width], a_bank[:], b_bank[:], b_sb[:, 0:width])
+            gated_product(h_single[:, s * T + lo : s * T + lo + width], a_bank[:], b_bank[:], b_sb[:, 0:width])
 
-        def pair_planes(j, lo):
+        def pair_planes(lo):
             b_bank = psum_b.tile([P, CHUNK], F32, name="b_bank")
             a_bank = psum_a.tile([P, CHUNK], F32, name="a_bank")
             for bank, code, scale in ((b_bank, w3_code, w3_scale), (a_bank, w1_code, w1_scale)):
                 for d in range(2):
-                    first_layer(bank[:, d * HALF : (d + 1) * HALF], code, scale, d, j, lo, HALF)
+                    first_layer(bank[:, d * HALF : (d + 1) * HALF], code, scale, d, lo, HALF)
             b_sb = ring.tile([P, CHUNK], F32, name="b_sb", align_bytes=64)
-            first = 2 * (j * CHUNK + lo)
-            gated(
-                h_pair[:, first : first + 2 * HALF].rearrange("p (n d) -> p n d", d=2),
+            gated_product(
+                h_pair[0][:, 2 * lo : 2 * (lo + HALF)].rearrange("p (n d) -> p n d", d=2),
                 a_bank[:].rearrange("p (d n) -> p n d", d=2),
                 b_bank[:].rearrange("p (d n) -> p n d", d=2),
                 b_sb[:].rearrange("p (n d) -> p n d", d=2),
             )
 
-        for j in range(T // CHUNK):
-            if j == 0:
-                single_plane(j, 0, 0, HALF)
-                single_plane(j, 0, HALF, HALF)
-            else:
-                single_plane(j, 0, 0, CHUNK)
-            single_plane(j, 1, 0, CHUNK)
-            pair_planes(j, 0)
-            pair_planes(j, HALF)
+        def pair_up(lo):
+            nc.gpsimd.tensor_copy(
+                out=h_pair[1][:, 2 * lo : 2 * (lo + CHUNK)].rearrange("p (n d) -> p n d", d=2),
+                in_=h_single[:].rearrange("p (d n) -> p n d", d=2)[:, lo : lo + CHUNK, :],
+            )
 
-        areas = keep.tile([P, VECTOR_AREAS + SCALAR_AREAS, 2 * C], BF16, name="areas", align_bytes=64)
+        for lo in range(0, T, CHUNK):
+            if lo == 0:
+                single_plane(0, 0, HALF)
+                single_plane(0, HALF, HALF)
+            else:
+                single_plane(0, lo, CHUNK)
+            single_plane(1, lo, CHUNK)
+            pair_up(lo)
+            pair_planes(lo)
+            pair_planes(lo + HALF)
+
         y_banks = {}
-        quads = [keep.tile([P, PACK * C], BF16, name="quads%d" % e, align_bytes=64) for e in range(E)]
-        h_code = [keep.tile([P, C], U32, name="h_code%d" % e, align_bytes=64) for e in range(E)]
+        quads = [areas[:, a * C : (a + 2) * C] for a in QUAD_AREA]
+        h_code = keep.tile([P, C], U32, name="h_code", align_bytes=64)
         h_scale = [keep.tile([P, C], U8, name="h_scale%d" % e, align_bytes=64) for e in range(E)]
         y_sb = [keep.tile([P, C], F32, name="y_sb%d" % e, align_bytes=64) for e in range(E)]
 
-        def slots(e, count=1):
-            return offsets[:, e * C // 16 : (e + count) * C // 16]
+        def area(a):
+            return areas[:, a * C : (a + 1) * C]
 
-        def gather_pairs(e, count):
+        def slots(e):
+            return offsets[:, e * C // 16 : (e + 1) * C // 16]
+
+        def gather(e, s):
             nc.vector.tensor_copy(
-                out=areas[:, AREA[e] : AREA[e] + count, :].rearrange("p a w -> p (a w)").bitcast(U32),
-                in_=h_pair[:].bitcast(U32).indirect(slots(e, count)),
+                out=area((LOW_AREA, HIGH_AREA)[s][e]), in_=h_pair[s][:].bitcast(U32).indirect(slots(e))
             )
 
-        def gather_single(e, s):
-            nc.scalar.activation(
-                out=areas[:, VECTOR_AREAS + e % SCALAR_AREAS, s : 2 * C : 2],
-                in_=h_single[s][:].indirect(slots(e)),
-                func=COPY,
-            )
+        def gather_singles(e):
+            for s in range(2):
+                nc.scalar.activation(
+                    out=area(HIGH_AREA[e]).bitcast(BF16)[:, s : 2 * C : 2],
+                    in_=h_single[:, s * T : (s + 1) * T].indirect(slots(e)),
+                    func=COPY,
+                )
 
         def interleave(e):
-            lo, hi = AREA[e], VECTOR_AREAS + e % SCALAR_AREAS
-            nc.scalar.copy(
-                out=quads[e][:].bitcast(U32).rearrange("p (u half) -> p u half", half=2),
-                in_=areas[:].bitcast(U32)[:, lo : hi + 1 : hi - lo, :].rearrange("p half u -> p u half"),
-            )
+            lo, hi = LOW_AREA[e], HIGH_AREA[e]
+            both = areas[:].rearrange("p (a u) -> p a u", u=C)[:, lo : hi + 1 : hi - lo, :]
+            both = both.rearrange("p half u -> p u half")
+            dst = quads[e].rearrange("p (u half) -> p u half", half=2)
+            if e == 0:
+                nc.scalar.copy(out=dst, in_=both)
+            else:
+                nc.gpsimd.tensor_copy(out=dst, in_=both)
 
         def quantise(e):
-            nc.vector.quantize_mx(out=h_code[e][:].bitcast(FP8X4), scales=h_scale[e][:], in_=quads[e][:])
-
-        def second_layer(e):
+            nc.vector.quantize_mx(out=h_code[:].bitcast(FP8X4), scales=h_scale[e][:], in_=quads[e].bitcast(BF16))
             y_bank = psum_b.tile([P, C], F32, name="b_bank")
             nc.tensor.matmul_mx(
                 out=y_bank[:],
                 lhsT=w2_code[:, e * 2 * N : (e + 1) * 2 * N].bitcast(FP4X4),
                 lhsT_scale=w2_scale[:, e * N : (e + 1) * N],
-                rhs=h_code[e][:].bitcast(FP8X4),
+                rhs=h_code[:].bitcast(FP8X4),
                 rhs_scale=h_scale[e][:],
                 start=True,
                 stop=True,
             )
             y_banks[e] = y_bank
 
-        def evacuate(e):
-            nc.scalar.activation(out=y_sb[e][:], in_=y_banks[e][:], func=COPY)
+        def put_back(e):
+            nc.vector.tensor_tensor(y_sb[e][:], y_banks[e][:], gate_sb[:, e * C : (e + 1) * C], ALU.mult)
+            nc.scalar.activation(out=result[:].indirect(slots(e)), in_=y_sb[e][:], func=COPY)
 
-        def scatter(e):
-            nc.vector.tensor_tensor(
-                result[:].indirect(slots(e)), y_sb[e][:], gate_sb[:, e * C : (e + 1) * C], ALU.mult
-            )
-
-        gather_single(0, 0)
-        gather_single(0, 1)
-        gather_pairs(0, 1)
-        gather_pairs(1, 1)
-        gather_pairs(2, 2)
-        for e in range(E + 1):
+        gather_singles(0)
+        gather(0, 0)
+        interleave(0)
+        gather(1, 0)
+        gather_singles(1)
+        interleave(1)
+        quantise(0)
+        gather(2, 0)
+        gather(2, 1)
+        interleave(2)
+        put_back(0)
+        quantise(1)
+        gather(3, 0)
+        put_back(1)
+        for e in range(2, E):
+            quantise(e)
             if e + 1 < E:
-                gather_single(e + 1, 0)
-            if e < E:
-                interleave(e)
-            if e < E:
-                quantise(e)
-                second_layer(e)
-            if e == 0:
-                gather_pairs(4, 2)
-            if e > 0:
-                evacuate(e - 1)
-                scatter(e - 1)
-            if e + 1 < E:
-                gather_single(e + 1, 1)
+                gather(e + 1, 1)
+                interleave(e + 1)
+            if e + 2 < E:
+                gather(e + 2, 0)
+            put_back(e)
 
         nc.sync.dma_start(out=out, in_=result[:])

@@ -22,10 +22,11 @@ QUADRANTS = 4
 CHUNK = 512
 HALF = CHUNK // 2
 W3_COPIES = 12
-QUAD_AREA = (7, 15, 2, 4, 17, 19)
+QUAD_AREA = (2, 4, 6, 15, 17, 19)
 GATE_AREA = 9
-LOW_AREA = (0, 1, 0, 1, QUAD_AREA[2], QUAD_AREA[3])
-HIGH_AREA = (6, 6, QUAD_AREA[0], GATE_AREA + 1, GATE_AREA + 2, GATE_AREA + 3)
+LOW_AREA = (0, 1, 0, QUAD_AREA[0], QUAD_AREA[1], QUAD_AREA[2])
+HIGH_AREA = (8, 8, QUAD_AREA[0] + 1, GATE_AREA, GATE_AREA + 1, GATE_AREA + 2)
+STORE_CUTS = (0, 256, 768, 1280, 1536)
 AREAS = 21
 BANKS = 4
 
@@ -58,6 +59,7 @@ def tile_moe_sup_glu_relu_kernel(
         gate_sb = areas[:, GATE_AREA * C : (GATE_AREA + E) * C].bitcast(F32)
         h_pair = [keep.tile([P, 2 * T], BF16, name="h_pair%d" % s, align_bytes=64) for s in range(2)]
         h_single = keep.tile([P, 2 * T], BF16, name="h_single", align_bytes=64)
+        window = [keep.tile([P, T], F32, name="window%d" % w, align_bytes=64) for w in range(2)]
         result = keep.tile([P, T], F32, name="result", align_bytes=64)
 
         def load_weight_scales(queue, tile_view, scales, q):
@@ -73,6 +75,8 @@ def tile_moe_sup_glu_relu_kernel(
         xw = words(x_words[0])
         nc.vector.memset(x_scale[:].bitcast(I32), 0)
         nc.vector.memset(w2_scale[:].bitcast(I32), 0)
+        for w in range(2):
+            nc.vector.memset(window[w][:].bitcast(I32), 0)
 
         for q in range(QUADRANTS):
             load_weight_scales(nc.scalar if q % 2 else nc.sync, w3_scale_raw, w3_scales[0], q)
@@ -188,8 +192,10 @@ def tile_moe_sup_glu_relu_kernel(
 
         y_banks = {}
         quads = [areas[:, a * C : (a + 2) * C] for a in QUAD_AREA]
-        h_code = keep.tile([P, C], U32, name="h_code", align_bytes=64)
-        h_scale = [keep.tile([P, C], U8, name="h_scale%d" % e, align_bytes=64) for e in range(E)]
+        codes = [keep.tile([P, C], U32, name="h_code%d" % b, align_bytes=64) for b in range(2)]
+        h_code = [codes[e == E - 1] for e in range(E)]
+        planes = [keep.tile([P, C], U8, name="h_scale%d" % b, align_bytes=64) for b in range(2)]
+        h_scale = [planes[e % 2] for e in range(E)]
         y_sb = [keep.tile([P, C], F32, name="y_sb%d" % e, align_bytes=64) for e in range(E)]
 
         def area(a):
@@ -222,13 +228,13 @@ def tile_moe_sup_glu_relu_kernel(
                 nc.gpsimd.tensor_copy(out=dst, in_=both)
 
         def quantise(e):
-            nc.vector.quantize_mx(out=h_code[:].bitcast(FP8X4), scales=h_scale[e][:], in_=quads[e].bitcast(BF16))
+            nc.vector.quantize_mx(out=h_code[e][:].bitcast(FP8X4), scales=h_scale[e][:], in_=quads[e].bitcast(BF16))
             y_bank = psum_b.tile([P, C], F32, name="b_bank")
             nc.tensor.matmul_mx(
                 out=y_bank[:],
                 lhsT=w2_code[:, e * 2 * N : (e + 1) * 2 * N].bitcast(FP4X4),
                 lhsT_scale=w2_scale[:, e * N : (e + 1) * N],
-                rhs=h_code[:].bitcast(FP8X4),
+                rhs=h_code[e][:].bitcast(FP8X4),
                 rhs_scale=h_scale[e][:],
                 start=True,
                 stop=True,
@@ -237,7 +243,11 @@ def tile_moe_sup_glu_relu_kernel(
 
         def put_back(e):
             nc.vector.tensor_tensor(y_sb[e][:], y_banks[e][:], gate_sb[:, e * C : (e + 1) * C], ALU.mult)
-            nc.scalar.activation(out=result[:].indirect(slots(e)), in_=y_sb[e][:], func=COPY)
+            target = window[e % 2][:].indirect(slots(e))
+            if e < E - 1:
+                nc.scalar.activation(out=target, in_=y_sb[e][:], func=COPY)
+            else:
+                nc.vector.tensor_copy(out=target, in_=y_sb[e][:])
 
         gather_singles(0)
         gather(0, 0)
@@ -247,19 +257,22 @@ def tile_moe_sup_glu_relu_kernel(
         interleave(1)
         quantise(0)
         gather(2, 0)
-        gather(2, 1)
+        gather_singles(2)
         interleave(2)
-        put_back(0)
-        quantise(1)
         gather(3, 0)
-        put_back(1)
-        for e in range(2, E):
+        put_back(0)
+        for e in range(1, E - 2):
             quantise(e)
-            if e + 1 < E:
-                gather(e + 1, 1)
-                interleave(e + 1)
-            if e + 2 < E:
-                gather(e + 2, 0)
+            gather(e + 2, 1)
+            interleave(e + 2)
+            if e + 3 < E:
+                gather(e + 3, 0)
+            put_back(e)
+        for e in range(E - 2, E):
+            quantise(e)
+        for e in range(E - 2, E):
             put_back(e)
 
-        nc.sync.dma_start(out=out, in_=result[:])
+        for lo, hi in zip(STORE_CUTS, STORE_CUTS[1:]):
+            nc.vector.tensor_tensor(result[:, lo:hi], window[0][:, lo:hi], window[1][:, lo:hi], ALU.add)
+            nc.sync.dma_start(out=out[:, lo:hi], in_=result[:, lo:hi])

@@ -22,7 +22,7 @@ QUADRANTS = 4
 CHUNK = 512
 HALF = CHUNK // 2
 W3_COPIES = 12
-QUAD_AREA = (2, 4, 6, 15, 17, 19)
+QUAD_AREA = (2, 4, 5, 15, 17, 19)
 GATE_AREA = 9
 LOW_AREA = (0, 1, 0, QUAD_AREA[0], QUAD_AREA[1], QUAD_AREA[2])
 HIGH_AREA = (8, 8, QUAD_AREA[0] + 1, GATE_AREA, GATE_AREA + 1, GATE_AREA + 2)
@@ -193,7 +193,7 @@ def tile_moe_sup_glu_relu_kernel(
         y_banks = {}
         quads = [areas[:, a * C : (a + 2) * C] for a in QUAD_AREA]
         codes = [keep.tile([P, C], U32, name="h_code%d" % b, align_bytes=64) for b in range(2)]
-        h_code = [codes[e == E - 1] for e in range(E)]
+        h_code = [codes[e == E - 2] for e in range(E)]
         planes = [keep.tile([P, C], U8, name="h_scale%d" % b, align_bytes=64) for b in range(2)]
         h_scale = [planes[e % 2] for e in range(E)]
         y_sb = [keep.tile([P, C], F32, name="y_sb%d" % e, align_bytes=64) for e in range(E)]
@@ -258,20 +258,24 @@ def tile_moe_sup_glu_relu_kernel(
         quantise(0)
         gather(2, 0)
         gather_singles(2)
-        interleave(2)
         gather(3, 0)
         put_back(0)
-        for e in range(1, E - 2):
+        for e in range(1, E - 3):
             quantise(e)
+            if e == 1:
+                interleave(2)
             gather(e + 2, 1)
             interleave(e + 2)
-            if e + 3 < E:
-                gather(e + 3, 0)
+            gather(e + 3, 0)
             put_back(e)
-        for e in range(E - 2, E):
-            quantise(e)
-        for e in range(E - 2, E):
-            put_back(e)
+        quantise(E - 3)
+        quantise(E - 2)
+        gather(E - 1, 1)
+        interleave(E - 1)
+        put_back(E - 3)
+        put_back(E - 2)
+        quantise(E - 1)
+        put_back(E - 1)
 
         for lo, hi in zip(STORE_CUTS, STORE_CUTS[1:]):
             nc.vector.tensor_tensor(result[:, lo:hi], window[0][:, lo:hi], window[1][:, lo:hi], ALU.add)

@@ -42,14 +42,14 @@ def tile_moe_sup_glu_relu_kernel(
         psum_b = ctx.enter_context(tc.psum_pool(name="psum_b", bufs=BANKS))
 
         offsets = keep.tile([P, T // 16], U16, name="offsets")
-        loaded_scales = keep.tile([P, 2 * H], U8, name="loaded_scales", align_bytes=64)
+        loaded_scales = keep.tile([P, 2 * H], U8, name="loaded_scales", tag="reused0", align_bytes=64)
         w1_scale_raw = loaded_scales[:, 0:H]
         w3_scale_raw = loaded_scales[:, H : 2 * H]
         x_scale = keep.tile([P, T], U8, name="x_scale", align_bytes=64)
         w1_scale = keep.tile([P, H], U8, name="w1_scale", align_bytes=64)
         w3_scale = keep.tile([P, H], U8, name="w3_scale", align_bytes=64)
         w2_scale = keep.tile([P, E * N], U8, name="w2_scale", align_bytes=64)
-        w1_raw = keep.tile([P, H], I32, name="w1_raw", align_bytes=64)
+        w1_raw = keep.tile([P, H], I32, name="w1_raw", tag="reused1", align_bytes=64)
         w3_raw = keep.tile([P, H], I32, name="w3_raw", align_bytes=64)
         w1_code = keep.tile([P, H], I32, name="w1_code", align_bytes=64)
         w3_code = keep.tile([P, H], I32, name="w3_code", align_bytes=64)
@@ -59,7 +59,6 @@ def tile_moe_sup_glu_relu_kernel(
         gate_sb = areas[:, GATE_AREA * C : (GATE_AREA + E) * C].bitcast(F32)
         h_pair = [keep.tile([P, 2 * T], BF16, name="h_pair%d" % s, align_bytes=64) for s in range(2)]
         h_single = keep.tile([P, 2 * T], BF16, name="h_single", align_bytes=64)
-        window = [keep.tile([P, T], F32, name="window%d" % w, align_bytes=64) for w in range(2)]
         result = keep.tile([P, T], F32, name="result", align_bytes=64)
 
         def load_weight_scales(queue, tile_view, scales, q):
@@ -75,8 +74,6 @@ def tile_moe_sup_glu_relu_kernel(
         xw = words(x_words[0])
         nc.vector.memset(x_scale[:].bitcast(I32), 0)
         nc.vector.memset(w2_scale[:].bitcast(I32), 0)
-        for w in range(2):
-            nc.vector.memset(window[w][:].bitcast(I32), 0)
 
         for q in range(QUADRANTS):
             load_weight_scales(nc.scalar if q % 2 else nc.sync, w3_scale_raw, w3_scales[0], q)
@@ -134,6 +131,10 @@ def tile_moe_sup_glu_relu_kernel(
                 start=True,
                 stop=True,
             )
+
+        window = [keep.tile([P, T], F32, name="window%d" % w, tag="reused%d" % w, align_bytes=64) for w in range(2)]
+        for w in range(2):
+            nc.gpsimd.memset(window[w][:].bitcast(I32), 0)
 
         def first_layer(bank, code, scale, d, lo, width):
             cols = slice(d * P, (d + 1) * P)

@@ -22,12 +22,13 @@ QUADRANTS = 4
 CHUNK = 512
 HALF = CHUNK // 2
 W3_COPIES = 12
-QUAD_AREA = (2, 4, 5, 15, 17, 19)
-GATE_AREA = 9
-LOW_AREA = (0, 1, 0, QUAD_AREA[0], QUAD_AREA[1], QUAD_AREA[2])
-HIGH_AREA = (8, 8, QUAD_AREA[0] + 1, GATE_AREA, GATE_AREA + 1, GATE_AREA + 2)
+QUAD_AREA = (3, 5, 6, 16, 18, 20)
+GATE_AREA = 10
+LOW_AREA = (0, QUAD_AREA[0] - 1, 0, 1, QUAD_AREA[1], QUAD_AREA[2])
+HIGH_AREA = (9, 9, QUAD_AREA[0], GATE_AREA, GATE_AREA + 1, GATE_AREA + 2)
+VECTOR_SLOTS = 320
 STORE_CUTS = (0, 256, 768, 1280, 1536)
-AREAS = 21
+AREAS = 22
 BANKS = 4
 
 
@@ -197,17 +198,19 @@ def tile_moe_sup_glu_relu_kernel(
         h_code = [codes[e == E - 2] for e in range(E)]
         planes = [keep.tile([P, C], U8, name="h_scale%d" % b, align_bytes=64) for b in range(2)]
         h_scale = [planes[e % 2] for e in range(E)]
-        y_sb = [keep.tile([P, C], F32, name="y_sb%d" % e, align_bytes=64) for e in range(E)]
+        y_sb = keep.tile([P, T], F32, name="y_sb", align_bytes=64)
 
         def area(a):
             return areas[:, a * C : (a + 1) * C]
 
-        def slots(e):
-            return offsets[:, e * C // 16 : (e + 1) * C // 16]
+        def slots(e, count=1):
+            return offsets[:, e * C // 16 : (e + count) * C // 16]
 
-        def gather(e, s):
+        def gather(e, s, count=1):
+            first = (LOW_AREA, HIGH_AREA)[s][e]
             nc.vector.tensor_copy(
-                out=area((LOW_AREA, HIGH_AREA)[s][e]), in_=h_pair[s][:].bitcast(U32).indirect(slots(e))
+                out=areas[:, first * C : (first + count) * C],
+                in_=h_pair[s][:].bitcast(U32).indirect(slots(e, count)),
             )
 
         def gather_singles(e):
@@ -225,6 +228,8 @@ def tile_moe_sup_glu_relu_kernel(
             dst = quads[e].rearrange("p (u half) -> p u half", half=2)
             if e == 0:
                 nc.scalar.copy(out=dst, in_=both)
+            elif e == E - 1:
+                nc.vector.tensor_copy(out=dst.bitcast(I32), in_=both.bitcast(I32))
             else:
                 nc.gpsimd.tensor_copy(out=dst, in_=both)
 
@@ -243,12 +248,16 @@ def tile_moe_sup_glu_relu_kernel(
             y_banks[e] = y_bank
 
         def put_back(e):
-            nc.vector.tensor_tensor(y_sb[e][:], y_banks[e][:], gate_sb[:, e * C : (e + 1) * C], ALU.mult)
-            target = window[e % 2][:].indirect(slots(e))
+            lo, hi = e * C, (e + 1) * C
+            nc.vector.tensor_tensor(y_sb[:, lo:hi], y_banks[e][:], gate_sb[:, lo:hi], ALU.mult)
             if e < E - 1:
-                nc.scalar.activation(out=target, in_=y_sb[e][:], func=COPY)
+                hi = min(hi, T - VECTOR_SLOTS)
+                target = window[e in (0, 2)][:].indirect(offsets[:, lo // 16 : hi // 16])
+                nc.scalar.activation(out=target, in_=y_sb[:, lo:hi], func=COPY)
             else:
-                nc.vector.tensor_copy(out=target, in_=y_sb[e][:])
+                lo = T - VECTOR_SLOTS
+                target = window[e % 2][:].indirect(offsets[:, lo // 16 : hi // 16])
+                nc.vector.tensor_copy(out=target, in_=y_sb[:, lo:hi])
 
         gather_singles(0)
         gather(0, 0)
@@ -257,9 +266,8 @@ def tile_moe_sup_glu_relu_kernel(
         gather_singles(1)
         interleave(1)
         quantise(0)
-        gather(2, 0)
+        gather(2, 0, 2)
         gather_singles(2)
-        gather(3, 0)
         put_back(0)
         for e in range(1, E - 3):
             quantise(e)
@@ -270,12 +278,12 @@ def tile_moe_sup_glu_relu_kernel(
             gather(e + 3, 0)
             put_back(e)
         quantise(E - 3)
-        quantise(E - 2)
         gather(E - 1, 1)
+        quantise(E - 2)
         interleave(E - 1)
         put_back(E - 3)
-        put_back(E - 2)
         quantise(E - 1)
+        put_back(E - 2)
         put_back(E - 1)
 
         for lo, hi in zip(STORE_CUTS, STORE_CUTS[1:]):

@@ -27,7 +27,7 @@ GATE_AREA = 10
 LOW_AREA = (0, QUAD_AREA[0] - 1, 0, 1, QUAD_AREA[1], QUAD_AREA[2])
 HIGH_AREA = (9, 9, QUAD_AREA[0], GATE_AREA, GATE_AREA + 1, GATE_AREA + 2)
 VECTOR_SLOTS = 320
-STORE_CUTS = (0, 256, 768, 1280, 1536)
+STORE_CUTS = (0, 512, 1024, 1536)
 AREAS = 22
 BANKS = 4
 
@@ -54,7 +54,9 @@ def tile_moe_sup_glu_relu_kernel(
         w3_raw = keep.tile([P, H], I32, name="w3_raw", align_bytes=64)
         w1_code = keep.tile([P, H], I32, name="w1_code", align_bytes=64)
         w3_code = keep.tile([P, H], I32, name="w3_code", align_bytes=64)
-        x_code = [keep.tile([P, CHUNK], I32, name="x_code%d" % j, align_bytes=64) for j in range(T // CHUNK)]
+        x_first = keep.tile([P, CHUNK], I32, name="x_first", align_bytes=64)
+        x_rest = keep.tile([P, T - CHUNK], I32, name="x_rest", align_bytes=64)
+        x_code = [x_first[:], x_rest[:, 0:CHUNK], x_rest[:, CHUNK : 2 * CHUNK]]
         w2_code = keep.tile([P, E * 2 * N], U8, name="w2_code", align_bytes=64)
         areas = keep.tile([P, AREAS * C], U32, name="areas", align_bytes=64)
         gate_sb = areas[:, GATE_AREA * C : (GATE_AREA + E) * C].bitcast(F32)
@@ -90,8 +92,7 @@ def tile_moe_sup_glu_relu_kernel(
                 out=x_scale[32 * q : 32 * q + 4, :].bitcast(I32), in_=x_scales[0][4 * q : 4 * q + 4, :].bitcast(I32)
             )
         nc.sync.dma_start(out=x_code[0][:, HALF:CHUNK], in_=xw[:, HALF:CHUNK])
-        for j in range(1, T // CHUNK):
-            nc.sync.dma_start(out=x_code[j][:], in_=xw[:, j * CHUNK : (j + 1) * CHUNK])
+        nc.sync.dma_start(out=x_rest[:], in_=xw[:, CHUNK:T])
 
         nc.sync.dma_start(offsets[:], offs)
         nc.sync.dma_start(
@@ -99,7 +100,7 @@ def tile_moe_sup_glu_relu_kernel(
             in_=w2_words.bitcast(I32).rearrange("e s p w -> p (e s) w"),
         )
         for q in range(QUADRANTS):
-            queue = nc.gpsimd if q == QUADRANTS - 1 else nc.sync
+            queue = nc.gpsimd if q >= QUADRANTS - 2 else nc.sync
             queue.dma_start(
                 out=w2_scale[32 * q : 32 * q + 4, :].bitcast(I32).rearrange("r (e w) -> r e w", e=E),
                 in_=w2_scales.bitcast(I32)[:, 0, 4 * q : 4 * q + 4, :].rearrange("e r w -> r e w"),

@@ -24,7 +24,7 @@ HALF = CHUNK // 2
 W3_COPIES = 12
 QUAD_AREA = (3, 5, 6, 16, 18, 20)
 GATE_AREA = 10
-LOW_AREA = (0, QUAD_AREA[0] - 1, 0, 1, QUAD_AREA[1], QUAD_AREA[2])
+LOW_AREA = (0, 1, 2, 0, QUAD_AREA[1], QUAD_AREA[2])
 HIGH_AREA = (9, 9, QUAD_AREA[0], GATE_AREA, GATE_AREA + 1, GATE_AREA + 2)
 VECTOR_SLOTS = 320
 STORE_CUTS = (0, 512, 1024, 1536)
@@ -263,11 +263,11 @@ def tile_moe_sup_glu_relu_kernel(
         gather_singles(0)
         gather(0, 0)
         interleave(0)
-        gather(1, 0)
+        gather(1, 0, 2)
         gather_singles(1)
         interleave(1)
         quantise(0)
-        gather(2, 0, 2)
+        gather(3, 0)
         gather_singles(2)
         put_back(0)
         for e in range(1, E - 3):

from contextlib import ExitStack

import concourse.mybir as mybir

K, T, E, C, H, N = 512, 1536, 6, 256, 512, 128
FLOPS = 2 * K * H * T * 2 + 2 * H * N * T

F32 = mybir.dt.float32
BF16 = mybir.dt.bfloat16
I32 = mybir.dt.int32
U32 = mybir.dt.uint32
U16 = mybir.dt.uint16
U8 = mybir.dt.uint8
FP8X4 = mybir.dt.float8_e4m3fn_x4
FP4X4 = mybir.dt.float4_e2m1fn_x4
ALU = mybir.AluOpType
COPY = mybir.ActivationFunctionType.Copy

P = 128
PACK = 4
QUADRANTS = 4
CHUNK = 512
HALF = CHUNK // 2
W3_COPIES = 12
QUAD_AREA = (3, 5, 6, 16, 18, 20)
GATE_AREA = 10
LOW_AREA = (0, 1, 2, 0, QUAD_AREA[1], QUAD_AREA[2])
HIGH_AREA = (9, 9, QUAD_AREA[0], GATE_AREA, GATE_AREA + 1, GATE_AREA + 2)
VECTOR_SLOTS = 320
STORE_CUTS = (0, 512, 1024, 1536)
AREAS = 22
BANKS = 4


def tile_moe_sup_glu_relu_kernel(
    tc, x_words, x_scales, w1_words, w1_scales, w3_words, w3_scales, w2_words, w2_scales, gate, offs, out
):
    nc = tc.nc
    with ExitStack() as ctx:
        keep = ctx.enter_context(tc.tile_pool(name="keep", bufs=1))
        ring = ctx.enter_context(tc.tile_pool(name="ring", bufs=W3_COPIES))
        psum_a = ctx.enter_context(tc.psum_pool(name="psum_a", bufs=BANKS))
        psum_b = ctx.enter_context(tc.psum_pool(name="psum_b", bufs=BANKS))

        offsets = keep.tile([P, T // 16], U16, name="offsets")
        loaded_scales = keep.tile([P, 2 * H], U8, name="loaded_scales", tag="reused0", align_bytes=64)
        w1_scale_raw = loaded_scales[:, 0:H]
        w3_scale_raw = loaded_scales[:, H : 2 * H]
        x_scale = keep.tile([P, T], U8, name="x_scale", align_bytes=64)
        w1_scale = keep.tile([P, H], U8, name="w1_scale", align_bytes=64)
        w3_scale = keep.tile([P, H], U8, name="w3_scale", align_bytes=64)
        w2_scale = keep.tile([P, E * N], U8, name="w2_scale", align_bytes=64)
        w1_raw = keep.tile([P, H], I32, name="w1_raw", tag="reused1", align_bytes=64)
        w3_raw = keep.tile([P, H], I32, name="w3_raw", align_bytes=64)
        w1_code = keep.tile([P, H], I32, name="w1_code", align_bytes=64)
        w3_code = keep.tile([P, H], I32, name="w3_code", align_bytes=64)
        x_first = keep.tile([P, CHUNK], I32, name="x_first", align_bytes=64)
        x_rest = keep.tile([P, T - CHUNK], I32, name="x_rest", align_bytes=64)
        x_code = [x_first[:], x_rest[:, 0:CHUNK], x_rest[:, CHUNK : 2 * CHUNK]]
        w2_code = keep.tile([P, E * 2 * N], U8, name="w2_code", align_bytes=64)
        areas = keep.tile([P, AREAS * C], U32, name="areas", align_bytes=64)
        gate_sb = areas[:, GATE_AREA * C : (GATE_AREA + E) * C].bitcast(F32)
        h_pair = [keep.tile([P, 2 * T], BF16, name="h_pair%d" % s, align_bytes=64) for s in range(2)]
        h_single = keep.tile([P, 2 * T], BF16, name="h_single", align_bytes=64)
        result = keep.tile([P, T], F32, name="result", align_bytes=64)

        def load_weight_scales(queue, tile_view, scales, q):
            rows = scales[4 * q : 4 * q + 4, :].bitcast(I32)
            queue.dma_start(
                out=tile_view[32 * q : 32 * q + 32, :].bitcast(I32),
                in_=rows.unsqueeze(0).to_broadcast([8, 4, rows.shape[1]]),
            )

        def words(ap):
            return ap.rearrange("p n d -> p (n d)").bitcast(I32)

        xw = words(x_words[0])
        nc.vector.memset(x_scale[:].bitcast(I32), 0)
        nc.vector.memset(w2_scale[:].bitcast(I32), 0)

        for q in range(QUADRANTS):
            load_weight_scales(nc.scalar if q % 2 else nc.sync, w3_scale_raw, w3_scales[0], q)
        load_weight_scales(nc.sync, w1_scale_raw, w1_scales[0], 0)
        load_weight_scales(nc.gpsimd, w1_scale_raw, w1_scales[0], 1)
        nc.sync.dma_start(out=x_code[0][:, 0:HALF], in_=xw[:, 0:HALF])
        nc.sync.dma_start(out=w3_raw[:], in_=words(w3_words[0]))
        nc.sync.dma_start(out=w1_raw[:], in_=words(w1_words[0]))
        for q in range(2, QUADRANTS):
            load_weight_scales(nc.sync, w1_scale_raw, w1_scales[0], q)
        for q in range(QUADRANTS):
            nc.sync.dma_start(
                out=x_scale[32 * q : 32 * q + 4, :].bitcast(I32), in_=x_scales[0][4 * q : 4 * q + 4, :].bitcast(I32)
            )
        nc.sync.dma_start(out=x_code[0][:, HALF:CHUNK], in_=xw[:, HALF:CHUNK])
        nc.sync.dma_start(out=x_rest[:], in_=xw[:, CHUNK:T])

        nc.sync.dma_start(offsets[:], offs)
        nc.sync.dma_start(
            out=w2_code[:].bitcast(I32).rearrange("p (e w) -> p e w", e=E),
            in_=w2_words.bitcast(I32).rearrange("e s p w -> p (e s) w"),
        )
        for q in range(QUADRANTS):
            queue = nc.gpsimd if q >= QUADRANTS - 2 else nc.sync
            queue.dma_start(
                out=w2_scale[32 * q : 32 * q + 4, :].bitcast(I32).rearrange("r (e w) -> r e w", e=E),
                in_=w2_scales.bitcast(I32)[:, 0, 4 * q : 4 * q + 4, :].rearrange("e r w -> r e w"),
            )
        nc.sync.dma_start(out=gate_sb, in_=gate)

        def reorder_words(dst, src):
            nc.vector.tensor_copy(
                out=dst.rearrange("p (d m) -> p m d", d=PACK), in_=src.rearrange("p (m d) -> p m d", d=PACK)
            )

        def reorder_scales(dst, src):
            nc.vector.tensor_copy(
                out=dst.rearrange("p (d m) -> p d m", d=PACK), in_=src.rearrange("p (m d) -> p d m", d=PACK)
            )

        reorder_scales(w3_scale[:], w3_scale_raw)
        reorder_words(w3_code[:], w3_raw[:])
        reorder_words(w1_code[:], w1_raw[:])
        reorder_scales(w1_scale[:], w1_scale_raw)

        warm_bank = psum_a.tile([P, CHUNK], F32, name="a_bank")
        for moving, width in ((x_code[0], HALF), (x_code[0], HALF), (x_code[0], HALF), (w3_raw, CHUNK)):
            nc.tensor.matmul_mx(
                out=warm_bank[:, 0:width],
                lhsT=x_code[0][:, 0:P].bitcast(FP8X4),
                lhsT_scale=w3_scale_raw[:, 0:P],
                rhs=moving[:, 0:width].bitcast(FP8X4),
                rhs_scale=w3_scale_raw[:, 0:width],
                start=True,
                stop=True,
            )

        window = [keep.tile([P, T], F32, name="window%d" % w, tag="reused%d" % w, align_bytes=64) for w in range(2)]
        for w in range(2):
            nc.gpsimd.memset(window[w][:].bitcast(I32), 0)

        def first_layer(bank, code, scale, d, lo, width):
            cols = slice(d * P, (d + 1) * P)
            nc.tensor.matmul_mx(
                out=bank,
                lhsT=code[:, cols].bitcast(FP8X4),
                lhsT_scale=scale[:, cols],
                rhs=x_code[lo // CHUNK][:, lo % CHUNK : lo % CHUNK + width].bitcast(FP8X4),
                rhs_scale=x_scale[:, lo : lo + width],
                start=True,
                stop=True,
            )

        def gated_product(dst, a_view, b_view, b_sb):
            nc.scalar.activation(out=b_sb, in_=b_view, func=COPY)
            nc.vector.scalar_tensor_tensor(out=dst, in0=a_view, scalar=0.0, in1=b_sb, op0=ALU.max, op1=ALU.mult)

        def single_plane(s, lo, width):
            b_bank = psum_b.tile([P, width], F32, name="b_bank")
            a_bank = psum_a.tile([P, width], F32, name="a_bank")
            for bank, code, scale in ((b_bank, w3_code, w3_scale), (a_bank, w1_code, w1_scale)):
                first_layer(bank[:], code, scale, 2 + s, lo, width)
            b_sb = ring.tile([P, CHUNK], F32, name="b_sb", align_bytes=64)
            gated_product(h_single[:, s * T + lo : s * T + lo + width], a_bank[:], b_bank[:], b_sb[:, 0:width])

        def pair_planes(lo):
            b_bank = psum_b.tile([P, CHUNK], F32, name="b_bank")
            a_bank = psum_a.tile([P, CHUNK], F32, name="a_bank")
            for bank, code, scale in ((b_bank, w3_code, w3_scale), (a_bank, w1_code, w1_scale)):
                for d in range(2):
                    first_layer(bank[:, d * HALF : (d + 1) * HALF], code, scale, d, lo, HALF)
            b_sb = ring.tile([P, CHUNK], F32, name="b_sb", align_bytes=64)
            gated_product(
                h_pair[0][:, 2 * lo : 2 * (lo + HALF)].rearrange("p (n d) -> p n d", d=2),
                a_bank[:].rearrange("p (d n) -> p n d", d=2),
                b_bank[:].rearrange("p (d n) -> p n d", d=2),
                b_sb[:].rearrange("p (n d) -> p n d", d=2),
            )

        def pair_up(lo):
            nc.gpsimd.tensor_copy(
                out=h_pair[1][:, 2 * lo : 2 * (lo + CHUNK)].rearrange("p (n d) -> p n d", d=2),
                in_=h_single[:].rearrange("p (d n) -> p n d", d=2)[:, lo : lo + CHUNK, :],
            )

        for lo in range(0, T, CHUNK):
            if lo == 0:
                single_plane(0, 0, HALF)
                single_plane(0, HALF, HALF)
            else:
                single_plane(0, lo, CHUNK)
            single_plane(1, lo, CHUNK)
            pair_up(lo)
            pair_planes(lo)
            pair_planes(lo + HALF)

        y_banks = {}
        quads = [areas[:, a * C : (a + 2) * C] for a in QUAD_AREA]
        codes = [keep.tile([P, C], U32, name="h_code%d" % b, align_bytes=64) for b in range(2)]
        h_code = [codes[e == E - 2] for e in range(E)]
        planes = [keep.tile([P, C], U8, name="h_scale%d" % b, align_bytes=64) for b in range(2)]
        h_scale = [planes[e % 2] for e in range(E)]
        y_sb = keep.tile([P, T], F32, name="y_sb", align_bytes=64)

        def area(a):
            return areas[:, a * C : (a + 1) * C]

        def slots(e, count=1):
            return offsets[:, e * C // 16 : (e + count) * C // 16]

        def gather(e, s, count=1):
            first = (LOW_AREA, HIGH_AREA)[s][e]
            nc.vector.tensor_copy(
                out=areas[:, first * C : (first + count) * C],
                in_=h_pair[s][:].bitcast(U32).indirect(slots(e, count)),
            )

        def gather_singles(e):
            for s in range(2):
                nc.scalar.activation(
                    out=area(HIGH_AREA[e]).bitcast(BF16)[:, s : 2 * C : 2],
                    in_=h_single[:, s * T : (s + 1) * T].indirect(slots(e)),
                    func=COPY,
                )

        def interleave(e):
            lo, hi = LOW_AREA[e], HIGH_AREA[e]
            both = areas[:].rearrange("p (a u) -> p a u", u=C)[:, lo : hi + 1 : hi - lo, :]
            both = both.rearrange("p half u -> p u half")
            dst = quads[e].rearrange("p (u half) -> p u half", half=2)
            if e == 0:
                nc.scalar.copy(out=dst, in_=both)
            elif e == E - 1:
                nc.vector.tensor_copy(out=dst.bitcast(I32), in_=both.bitcast(I32))
            else:
                nc.gpsimd.tensor_copy(out=dst, in_=both)

        def quantise(e):
            nc.vector.quantize_mx(out=h_code[e][:].bitcast(FP8X4), scales=h_scale[e][:], in_=quads[e].bitcast(BF16))
            y_bank = psum_b.tile([P, C], F32, name="b_bank")
            nc.tensor.matmul_mx(
                out=y_bank[:],
                lhsT=w2_code[:, e * 2 * N : (e + 1) * 2 * N].bitcast(FP4X4),
                lhsT_scale=w2_scale[:, e * N : (e + 1) * N],
                rhs=h_code[e][:].bitcast(FP8X4),
                rhs_scale=h_scale[e][:],
                start=True,
                stop=True,
            )
            y_banks[e] = y_bank

        def put_back(e):
            lo, hi = e * C, (e + 1) * C
            nc.vector.tensor_tensor(y_sb[:, lo:hi], y_banks[e][:], gate_sb[:, lo:hi], ALU.mult)
            if e < E - 1:
                hi = min(hi, T - VECTOR_SLOTS)
                target = window[e in (0, 2)][:].indirect(offsets[:, lo // 16 : hi // 16])
                nc.scalar.activation(out=target, in_=y_sb[:, lo:hi], func=COPY)
            else:
                lo = T - VECTOR_SLOTS
                target = window[e % 2][:].indirect(offsets[:, lo // 16 : hi // 16])
                nc.vector.tensor_copy(out=target, in_=y_sb[:, lo:hi])

        gather_singles(0)
        gather(0, 0)
        interleave(0)
        gather(1, 0, 2)
        gather_singles(1)
        interleave(1)
        quantise(0)
        gather(3, 0)
        gather_singles(2)
        put_back(0)
        for e in range(1, E - 3):
            quantise(e)
            if e == 1:
                interleave(2)
            gather(e + 2, 1)
            interleave(e + 2)
            gather(e + 3, 0)
            put_back(e)
        quantise(E - 3)
        gather(E - 1, 1)
        quantise(E - 2)
        interleave(E - 1)
        put_back(E - 3)
        quantise(E - 1)
        put_back(E - 2)
        put_back(E - 1)

        for lo, hi in zip(STORE_CUTS, STORE_CUTS[1:]):
            nc.vector.tensor_tensor(result[:, lo:hi], window[0][:, lo:hi], window[1][:, lo:hi], ALU.add)
            nc.sync.dma_start(out=out[:, lo:hi], in_=result[:, lo:hi])
